import numpy as np
import ml_dtypes


def mxq(x, axis, fmt="e4m3"):
    dtype, down = {"e4m3": (ml_dtypes.float8_e4m3fn, 7), "e5m2": (ml_dtypes.float8_e5m2, 14)}[fmt]
    v = np.moveaxis(np.asarray(x, np.float32).astype(ml_dtypes.bfloat16).astype(np.float64), axis, -1)
    blocks = v.reshape(v.shape[:-1] + (-1, 32))
    amax = np.abs(blocks).max(-1, keepdims=True)
    byte = np.maximum(np.where(amax > 0, np.frexp(amax)[1] - 1 + 127, 0) - down, 1)
    scale = np.exp2(byte - 127.0)
    codes = (blocks / scale).astype(np.float32).astype(dtype).astype(np.float64)
    return np.moveaxis((codes * scale).reshape(v.shape), -1, axis)


WIDE = False


def mx_kscale(k):
    if not WIDE:
        return np.ones(k)
    levels = np.array([10, -10, 5, -5, 0])
    if k % 512:
        return np.exp2(np.random.permutation(np.resize(levels, k // 32))).repeat(32)
    a = np.empty((k // 512, 16))
    for p in range(k // 512):
        a[p, :8] = np.random.permutation(np.resize(levels, 8))
        for g in range(8):
            far = levels[np.abs(levels - a[p, g]) >= 10]
            a[p, g + 8] = far[np.random.randint(len(far))]
    return np.exp2(a.ravel()).repeat(32)


def f64(x):
    return np.asarray(x).astype(np.float64)


def striped(idx):
    return np.tile(idx.reshape(-1, 16).T, (8, 1)).astype(np.uint16)


def unstriped(offs):
    return offs[:16].T.reshape(-1).astype(np.int64)


def relu(v):
    return np.maximum(v, 0.0)


def sigmoid(v):
    return 1.0 / (1.0 + np.exp(-np.maximum(v, -700.0)))


K, T, S, N, U = 1024, 1024, 512, 256, 1024


def setup_inputs():
    n = np.random.standard_normal
    s = mx_kscale(K)[:, None]
    return {
        "xT": (n((K, T)) * s).astype(np.float32),
        "mem": n((N, U)).astype(np.float32),
        "w1": (n((K, N)) / np.sqrt(K) / s).astype(np.float32),
        "w2": (n((K, N)) / np.sqrt(K) / s).astype(np.float32),
        "offs": striped(np.random.permutation(T)[:S]),
        "slot": striped(np.random.permutation(U)[:S]),
    }


def reference(xT, mem, w1, w2, offs, slot):
    old = f64(mem)[:, unstriped(slot)]
    xq = mxq(f64(xT)[:, unstriped(offs)], 0, "e4m3")
    g = sigmoid(mxq(f64(w2), 0, "e4m3").T @ xq)
    y = relu(mxq(f64(w1), 0, "e4m3").T @ xq)
    out = f64(mem).copy()
    out[:, unstriped(slot)] = old + g * (y - old)
    return out

@@ -1,0 +1,179 @@
+from contextlib import ExitStack
+
+import concourse.mybir as mybir
+
+K, T, S, N, U = 1024, 1024, 512, 256, 1024
+FLOPS = 2 * 2 * K * N * S
+
+F32 = mybir.dt.float32
+BF16 = mybir.dt.bfloat16
+I32 = mybir.dt.int32
+U32 = mybir.dt.uint32
+U16 = mybir.dt.uint16
+U8 = mybir.dt.uint8
+FP8X4 = mybir.dt.float8_e4m3fn_x4
+ACT = mybir.ActivationFunctionType
+ALU = mybir.AluOpType
+
+P = 128
+PACK = 4
+K_PASS = P * PACK
+PASSES = K // K_PASS
+BLOCKS = N // P
+X_CHUNKS = [[256, 256, 256, 256], [256, 256, 256, 128, 128]]
+X_ON_VECTOR = {(0, 0), (0, 3), (1, 3), (1, 4)}
+
+
+def interleave(nc, on_vector, grouped, raw):
+    dst = grouped.rearrange("p (c i) t -> p c t i", i=4)
+    src = raw.rearrange("p t (c i) -> p c t i", i=4)
+    if on_vector:
+        nc.vector.tensor_copy(out=dst, in_=src)
+    else:
+        nc.scalar.activation(out=dst, in_=src, func=ACT.Copy)
+
+
+def tile_picked_gmem_relu_e_kernel(tc, xT, mem, w1, w2, offs, slot, out):
+    nc = tc.nc
+    with ExitStack() as ctx:
+        keep = ctx.enter_context(tc.tile_pool(name="keep", bufs=1))
+        psum = ctx.enter_context(tc.psum_pool(name="psum", bufs=1))
+
+        offs_sb = keep.tile([P, S // 16], U16, name="offs_sb")
+        slot_sb = keep.tile([P, S // 16], U16, name="slot_sb")
+
+        x_words = [keep.tile([P, T], U32, name="x_words%d" % z, align_bytes=64) for z in range(PASSES)]
+        x_scales = [keep.tile([P, T], U8, name="x_scales%d" % z, align_bytes=64) for z in range(PASSES)]
+        for z in range(PASSES):
+            nc.vector.memset(x_scales[z][:].bitcast(I32), 0)
+
+        warm = keep.tile([P, 2], F32, name="warm")
+        nc.vector.memset(warm[:, 0:1], 0.0)
+        nc.scalar.activation(out=warm[:, 1:2], in_=warm[:, 0:1], func=ACT.Sigmoid)
+
+        x_raw = {}
+        for z in range(PASSES):
+            rows = xT[z * K_PASS : (z + 1) * K_PASS, :].rearrange("(p j) t -> p j t", j=PACK)
+            c0 = 0
+            for c, width in enumerate(X_CHUNKS[z]):
+                raw = keep.tile([P, PACK, width], F32, name="x_raw%d_%d" % (z, c))
+                nc.sync.dma_start(out=raw[:], in_=rows[:, :, c0 : c0 + width])
+                x_raw[z, c] = raw
+                c0 += width
+            if z == 0:
+                nc.sync.dma_start(offs_sb[:], offs)
+                nc.sync.dma_start(slot_sb[:], slot)
+        w_raw = {}
+        mem_sb = []
+        for b in range(BLOCKS):
+            for z in range(PASSES):
+                for m, w in enumerate((w2, w1)):
+                    raw = keep.tile([P, PACK, P], F32, name="w_raw%d_%d_%d" % (b, z, m))
+                    rows = w[z * K_PASS : (z + 1) * K_PASS, b * P : (b + 1) * P]
+                    nc.sync.dma_start(out=raw[:], in_=rows.rearrange("(p j) c -> p j c", j=PACK))
+                    w_raw[b, z, m] = raw
+            mem_b = keep.tile([P, U], F32, name="mem%d" % b)
+            nc.sync.dma_start(out=mem_b[:], in_=mem[b * P : (b + 1) * P, :])
+            mem_sb.append(mem_b)
+
+        picked_words = []
+        picked_scales = []
+
+        def quantise_messages(z):
+            c0 = 0
+            for c, width in enumerate(X_CHUNKS[z]):
+                grouped = keep.tile([P, width, PACK], BF16, name="x_grouped%d_%d" % (z, c), align_bytes=64)
+                interleave(nc, (z, c) in X_ON_VECTOR, grouped[:], x_raw[z, c][:])
+                nc.vector.quantize_mx(
+                    out=x_words[z][:, c0 : c0 + width].bitcast(FP8X4),
+                    scales=x_scales[z][:, c0 : c0 + width],
+                    in_=grouped[:].rearrange("p c t -> p (c t)"),
+                )
+                c0 += width
+
+        def pick_words(z):
+            words = keep.tile([P, S], U32, name="picked_words%d" % z, align_bytes=64)
+            nc.vector.tensor_copy(out=words[:], in_=x_words[z][:].indirect(offs_sb[:]))
+            picked_words.append(words)
+
+        def pick_scales(z, tag):
+            scales = keep.tile([P, S], U8, name="picked_scales%d" % z, tag=tag, align_bytes=64)
+            nc.vector.tensor_copy(out=scales[:], in_=x_scales[z][:].indirect(offs_sb[:]))
+            picked_scales.append(scales)
+
+        w_words = [keep.tile([P, PASSES, 2 * P], U32, name="w_words%d" % b, align_bytes=64) for b in range(BLOCKS)]
+        w_scales = [keep.tile([P, PASSES, 2 * P], U8, name="w_scales%d" % b, align_bytes=64) for b in range(BLOCKS)]
+
+        def quantise_weights(b, z, tag):
+            grouped = keep.tile([P, 2 * P, PACK], BF16, name="w_grouped%d_%d" % (b, z), tag=tag, align_bytes=64)
+            for m in range(2):
+                interleave(nc, False, grouped[:, m * P : (m + 1) * P, :], w_raw[b, z, m][:])
+            nc.vector.quantize_mx(
+                out=w_words[b][:, z, :].bitcast(FP8X4),
+                scales=w_scales[b][:, z, :],
+                in_=grouped[:].rearrange("p c t -> p (c t)"),
+            )
+
+        acc = {(b, m): psum.tile([P, S], F32, name="acc%d_%d" % (b, m)) for b in range(BLOCKS) for m in range(2)}
+
+        def product(b, m, z):
+            cols = slice(m * P, (m + 1) * P)
+            nc.tensor.matmul_mx(
+                out=acc[b, m][:],
+                lhsT=w_words[b][:, z, cols].bitcast(FP8X4),
+                lhsT_scale=w_scales[b][:, z, cols],
+                rhs=picked_words[z][:].bitcast(FP8X4),
+                rhs_scale=picked_scales[z][:],
+                start=(z == 0),
+                stop=(z == PASSES - 1),
+            )
+
+        def write_half(old, dist, gate, h, tag):
+            lo, hi = h * S // 2, (h + 1) * S // 2
+            step = keep.tile([P, S // 2], F32, name="step%d" % h, tag=tag, align_bytes=64)
+            nc.vector.tensor_tensor(step[:], dist[:, lo:hi], gate[:, lo:hi], ALU.mult)
+            nc.vector.tensor_tensor(
+                mem_sb[0][:].indirect(slot_sb[:, lo // 16 : hi // 16]), step[:], old[:, lo:hi], ALU.add
+            )
+
+        quantise_messages(0)
+        pick_words(0)
+        pick_scales(0, "picked_scales0")
+        quantise_messages(1)
+        pick_words(1)
+        quantise_weights(0, 0, "hold_a")
+        product(0, 0, 0)
+        product(0, 1, 0)
+        pick_scales(1, "hold_a")
+        quantise_weights(0, 1, "hold_b")
+        product(0, 0, 1)
+        product(0, 1, 1)
+        gate0 = keep.tile([P, S], F32, name="gate0")
+        nc.scalar.activation(out=gate0[:], in_=acc[0, 0][:], func=ACT.Sigmoid)
+        old = keep.tile([P, S], F32, name="old", tag="hold_b", align_bytes=64)
+        nc.vector.tensor_copy(out=old[:], in_=mem_sb[0][:].indirect(slot_sb[:]))
+        dist = keep.tile([P, S], F32, name="dist")
+        nc.vector.scalar_tensor_tensor(
+            out=dist[:], in0=acc[0, 1][:], scalar=0.0, in1=old[:], op0=ALU.max, op1=ALU.subtract
+        )
+        write_half(old, dist, gate0, 0, "step0")
+        quantise_weights(1, 0, "w_grouped1_0")
+        quantise_weights(1, 1, "hold_c")
+        for m in range(2):
+            for z in range(PASSES):
+                product(1, m, z)
+        write_half(old, dist, gate0, 1, "hold_c")
+        nc.sync.dma_start(out=out[0:P, :], in_=mem_sb[0][:])
+
+        rest1 = keep.tile([P, S], F32, name="rest1")
+        gate1 = keep.tile([P, S], F32, name="gate1")
+        nc.scalar.activation(out=rest1[:], in_=acc[1, 0][:], func=ACT.Sigmoid, scale=-1.0)
+        nc.scalar.activation(out=gate1[:], in_=acc[1, 0][:], func=ACT.Sigmoid)
+        kept = keep.tile([P, S], F32, name="kept")
+        fresh = keep.tile([P, S], F32, name="fresh")
+        nc.vector.tensor_tensor(kept[:], mem_sb[1][:].indirect(slot_sb[:]), rest1[:], ALU.mult)
+        nc.vector.scalar_tensor_tensor(
+            out=fresh[:], in0=acc[1, 1][:], scalar=0.0, in1=gate1[:], op0=ALU.max, op1=ALU.mult
+        )
+        nc.vector.tensor_tensor(mem_sb[1][:].indirect(slot_sb[:]), kept[:], fresh[:], ALU.add)
+        nc.sync.dma_start(out=out[P : 2 * P, :], in_=mem_sb[1][:])

@@ -7,7 +7,6 @@ FLOPS = 2 * 2 * K * N * S
 
 F32 = mybir.dt.float32
 BF16 = mybir.dt.bfloat16
-I32 = mybir.dt.int32
 U32 = mybir.dt.uint32
 U16 = mybir.dt.uint16
 U8 = mybir.dt.uint8
@@ -20,8 +19,6 @@ PACK = 4
 K_PASS = P * PACK
 PASSES = K // K_PASS
 BLOCKS = N // P
-X_CHUNKS = [[256, 256, 256, 256], [256, 256, 256, 128, 128]]
-X_ON_VECTOR = {(0, 0), (0, 3), (1, 3), (1, 4)}
 
 
 def interleave(nc, on_vector, grouped, raw):
@@ -42,11 +39,6 @@ def tile_picked_gmem_relu_e_kernel(tc, xT, mem, w1, w2, offs, slot, out):
         offs_sb = keep.tile([P, S // 16], U16, name="offs_sb")
         slot_sb = keep.tile([P, S // 16], U16, name="slot_sb")
 
-        x_words = [keep.tile([P, T], U32, name="x_words%d" % z, align_bytes=64) for z in range(PASSES)]
-        x_scales = [keep.tile([P, T], U8, name="x_scales%d" % z, align_bytes=64) for z in range(PASSES)]
-        for z in range(PASSES):
-            nc.vector.memset(x_scales[z][:].bitcast(I32), 0)
-
         warm = keep.tile([P, 2], F32, name="warm")
         nc.vector.memset(warm[:, 0:1], 0.0)
         nc.scalar.activation(out=warm[:, 1:2], in_=warm[:, 0:1], func=ACT.Sigmoid)
@@ -54,15 +46,13 @@ def tile_picked_gmem_relu_e_kernel(tc, xT, mem, w1, w2, offs, slot, out):
         x_raw = {}
         for z in range(PASSES):
             rows = xT[z * K_PASS : (z + 1) * K_PASS, :].rearrange("(p j) t -> p j t", j=PACK)
-            c0 = 0
-            for c, width in enumerate(X_CHUNKS[z]):
-                raw = keep.tile([P, PACK, width], F32, name="x_raw%d_%d" % (z, c))
-                nc.sync.dma_start(out=raw[:], in_=rows[:, :, c0 : c0 + width])
-                x_raw[z, c] = raw
-                c0 += width
-            if z == 0:
-                nc.sync.dma_start(offs_sb[:], offs)
-                nc.sync.dma_start(slot_sb[:], slot)
+            for j in range(PACK):
+                raw = keep.tile([P, T], F32, name="x_raw%d_%d" % (z, j))
+                nc.sync.dma_start(out=raw[:], in_=rows[:, j, :])
+                x_raw[z, j] = raw
+                if (z, j) == (0, 0):
+                    nc.sync.dma_start(offs_sb[:], offs)
+        nc.sync.dma_start(slot_sb[:], slot)
         w_raw = {}
         mem_sb = []
         for b in range(BLOCKS):
@@ -79,39 +69,38 @@ def tile_picked_gmem_relu_e_kernel(tc, xT, mem, w1, w2, offs, slot, out):
         picked_words = []
         picked_scales = []
 
-        def quantise_messages(z):
-            c0 = 0
-            for c, width in enumerate(X_CHUNKS[z]):
-                grouped = keep.tile([P, width, PACK], BF16, name="x_grouped%d_%d" % (z, c), align_bytes=64)
-                interleave(nc, (z, c) in X_ON_VECTOR, grouped[:], x_raw[z, c][:])
-                nc.vector.quantize_mx(
-                    out=x_words[z][:, c0 : c0 + width].bitcast(FP8X4),
-                    scales=x_scales[z][:, c0 : c0 + width],
-                    in_=grouped[:].rearrange("p c t -> p (c t)"),
-                )
-                c0 += width
+        def pick(z):
+            planes = keep.tile([P, PACK, S], BF16, name="planes%d" % z)
+            for j in range(PACK):
+                nc.vector.tensor_copy(out=planes[:, j, :], in_=x_raw[z, j][:].indirect(offs_sb[:]))
+            grouped = keep.tile([P, S, PACK], BF16, name="x_grouped%d" % z, align_bytes=64)
+            interleave(nc, z == PASSES - 1, grouped[:], planes[:])
+            return grouped
 
-        def pick_words(z):
+        def quantise_messages(z, grouped, tag):
             words = keep.tile([P, S], U32, name="picked_words%d" % z, align_bytes=64)
-            nc.vector.tensor_copy(out=words[:], in_=x_words[z][:].indirect(offs_sb[:]))
-            picked_words.append(words)
-
-        def pick_scales(z, tag):
             scales = keep.tile([P, S], U8, name="picked_scales%d" % z, tag=tag, align_bytes=64)
-            nc.vector.tensor_copy(out=scales[:], in_=x_scales[z][:].indirect(offs_sb[:]))
+            nc.vector.quantize_mx(
+                out=words[:].bitcast(FP8X4), scales=scales[:], in_=grouped[:].rearrange("p c t -> p (c t)")
+            )
+            picked_words.append(words)
             picked_scales.append(scales)
 
         w_words = [keep.tile([P, PASSES, 2 * P], U32, name="w_words%d" % b, align_bytes=64) for b in range(BLOCKS)]
         w_scales = [keep.tile([P, PASSES, 2 * P], U8, name="w_scales%d" % b, align_bytes=64) for b in range(BLOCKS)]
 
-        def quantise_weights(b, z, tag):
-            grouped = keep.tile([P, 2 * P, PACK], BF16, name="w_grouped%d_%d" % (b, z), tag=tag, align_bytes=64)
-            for m in range(2):
-                interleave(nc, False, grouped[:, m * P : (m + 1) * P, :], w_raw[b, z, m][:])
+        def quantise_weights(b, passes, tag):
+            grouped = keep.tile(
+                [P, len(passes), 2 * P, PACK], BF16, name="w_grouped%d_%d" % (b, passes[0]), tag=tag, align_bytes=64
+            )
+            for i, z in enumerate(passes):
+                for m in range(2):
+                    interleave(nc, False, grouped[:, i, m * P : (m + 1) * P, :], w_raw[b, z, m][:])
+            zs = slice(passes[0], passes[-1] + 1)
             nc.vector.quantize_mx(
-                out=w_words[b][:, z, :].bitcast(FP8X4),
-                scales=w_scales[b][:, z, :],
-                in_=grouped[:].rearrange("p c t -> p (c t)"),
+                out=w_words[b][:, zs, :].rearrange("p z c -> p (z c)").bitcast(FP8X4),
+                scales=w_scales[b][:, zs, :].rearrange("p z c -> p (z c)"),
+                in_=grouped[:].rearrange("p z c t -> p (z c t)"),
             )
 
         acc = {(b, m): psum.tile([P, S], F32, name="acc%d_%d" % (b, m)) for b in range(BLOCKS) for m in range(2)}
@@ -128,37 +117,40 @@ def tile_picked_gmem_relu_e_kernel(tc, xT, mem, w1, w2, offs, slot, out):
                 stop=(z == PASSES - 1),
             )
 
-        def write_half(old, dist, gate, h, tag):
-            lo, hi = h * S // 2, (h + 1) * S // 2
-            step = keep.tile([P, S // 2], F32, name="step%d" % h, tag=tag, align_bytes=64)
-            nc.vector.tensor_tensor(step[:], dist[:, lo:hi], gate[:, lo:hi], ALU.mult)
-            nc.vector.tensor_tensor(
-                mem_sb[0][:].indirect(slot_sb[:, lo // 16 : hi // 16]), step[:], old[:, lo:hi], ALU.add
-            )
+        halves = [slice(h * S // 2, (h + 1) * S // 2) for h in range(2)]
+        slot_halves = [slot_sb[:, h * S // 32 : (h + 1) * S // 32] for h in range(2)]
 
-        quantise_messages(0)
-        pick_words(0)
-        pick_scales(0, "picked_scales0")
-        quantise_messages(1)
-        pick_words(1)
-        quantise_weights(0, 0, "hold_a")
+        def write_half(old, dist, gate, h, tag):
+            step = keep.tile([P, S // 2], F32, name="step%d" % h, tag=tag, align_bytes=64)
+            nc.vector.tensor_tensor(step[:], dist[:, halves[h]], gate[:, halves[h]], ALU.mult)
+            nc.vector.tensor_tensor(mem_sb[0][:].indirect(slot_halves[h]), step[:], old[:, halves[h]], ALU.add)
+
+        quantise_messages(0, pick(0), "picked_scales0")
+        grouped1 = pick(1)
+        quantise_weights(0, [0], "hold_a")
         product(0, 0, 0)
         product(0, 1, 0)
-        pick_scales(1, "hold_a")
-        quantise_weights(0, 1, "hold_b")
+        quantise_messages(1, grouped1, "hold_a")
+        quantise_weights(0, [1], "hold_b")
         product(0, 0, 1)
         product(0, 1, 1)
         gate0 = keep.tile([P, S], F32, name="gate0")
         nc.scalar.activation(out=gate0[:], in_=acc[0, 0][:], func=ACT.Sigmoid)
         old = keep.tile([P, S], F32, name="old", tag="hold_b", align_bytes=64)
-        nc.vector.tensor_copy(out=old[:], in_=mem_sb[0][:].indirect(slot_sb[:]))
         dist = keep.tile([P, S], F32, name="dist")
-        nc.vector.scalar_tensor_tensor(
-            out=dist[:], in0=acc[0, 1][:], scalar=0.0, in1=old[:], op0=ALU.max, op1=ALU.subtract
-        )
+        for h in range(2):
+            nc.vector.tensor_copy(out=old[:, halves[h]], in_=mem_sb[0][:].indirect(slot_halves[h]))
+        for h in range(2):
+            nc.vector.scalar_tensor_tensor(
+                out=dist[:, halves[h]],
+                in0=acc[0, 1][:, halves[h]],
+                scalar=0.0,
+                in1=old[:, halves[h]],
+                op0=ALU.max,
+                op1=ALU.subtract,
+            )
         write_half(old, dist, gate0, 0, "step0")
-        quantise_weights(1, 0, "w_grouped1_0")
-        quantise_weights(1, 1, "hold_c")
+        quantise_weights(1, [0, 1], "hold_c")
         for m in range(2):
             for z in range(PASSES):
                 product(1, m, z)
@@ -172,8 +164,17 @@ def tile_picked_gmem_relu_e_kernel(tc, xT, mem, w1, w2, offs, slot, out):
         kept = keep.tile([P, S], F32, name="kept")
         fresh = keep.tile([P, S], F32, name="fresh")
         nc.vector.tensor_tensor(kept[:], mem_sb[1][:].indirect(slot_sb[:]), rest1[:], ALU.mult)
-        nc.vector.scalar_tensor_tensor(
-            out=fresh[:], in0=acc[1, 1][:], scalar=0.0, in1=gate1[:], op0=ALU.max, op1=ALU.mult
-        )
-        nc.vector.tensor_tensor(mem_sb[1][:].indirect(slot_sb[:]), kept[:], fresh[:], ALU.add)
+        for h in range(2):
+            nc.vector.scalar_tensor_tensor(
+                out=fresh[:, halves[h]],
+                in0=acc[1, 1][:, halves[h]],
+                scalar=0.0,
+                in1=gate1[:, halves[h]],
+                op0=ALU.max,
+                op1=ALU.mult,
+            )
+        for h in range(2):
+            nc.vector.tensor_tensor(
+                mem_sb[1][:].indirect(slot_halves[h]), kept[:, halves[h]], fresh[:, halves[h]], ALU.add
+            )
         nc.sync.dma_start(out=out[P : 2 * P, :], in_=mem_sb[1][:])

@@ -39,32 +39,31 @@ def tile_picked_gmem_relu_e_kernel(tc, xT, mem, w1, w2, offs, slot, out):
         offs_sb = keep.tile([P, S // 16], U16, name="offs_sb")
         slot_sb = keep.tile([P, S // 16], U16, name="slot_sb")
 
-        warm = keep.tile([P, 2], F32, name="warm")
-        nc.vector.memset(warm[:, 0:1], 0.0)
-        nc.scalar.activation(out=warm[:, 1:2], in_=warm[:, 0:1], func=ACT.Sigmoid)
-
         x_raw = {}
         for z in range(PASSES):
             rows = xT[z * K_PASS : (z + 1) * K_PASS, :].rearrange("(p j) t -> p j t", j=PACK)
             for j in range(PACK):
-                raw = keep.tile([P, T], F32, name="x_raw%d_%d" % (z, j))
+                raw = keep.tile([P, T], F32, name="x_raw%d_%d" % (z, j), align_bytes=64)
                 nc.sync.dma_start(out=raw[:], in_=rows[:, j, :])
                 x_raw[z, j] = raw
                 if (z, j) == (0, 0):
                     nc.sync.dma_start(offs_sb[:], offs)
-        nc.sync.dma_start(slot_sb[:], slot)
         w_raw = {}
         mem_sb = []
         for b in range(BLOCKS):
-            for z in range(PASSES):
-                for m, w in enumerate((w2, w1)):
-                    raw = keep.tile([P, PACK, P], F32, name="w_raw%d_%d_%d" % (b, z, m))
-                    rows = w[z * K_PASS : (z + 1) * K_PASS, b * P : (b + 1) * P]
-                    nc.sync.dma_start(out=raw[:], in_=rows.rearrange("(p j) c -> p j c", j=PACK))
-                    w_raw[b, z, m] = raw
+            pieces = [(z, m) for z in range(PASSES) for m in range(2)]
+            if b == 1:
+                pieces = [(z, m) for m in range(2) for z in range(PASSES)]
+            for z, m in pieces:
+                raw = keep.tile([P, PACK, P], F32, name="w_raw%d_%d_%d" % (b, z, m))
+                rows = (w2, w1)[m][z * K_PASS : (z + 1) * K_PASS, b * P : (b + 1) * P]
+                nc.sync.dma_start(out=raw[:], in_=rows.rearrange("(p j) c -> p j c", j=PACK))
+                w_raw[b, z, m] = raw
             mem_b = keep.tile([P, U], F32, name="mem%d" % b)
             nc.sync.dma_start(out=mem_b[:], in_=mem[b * P : (b + 1) * P, :])
             mem_sb.append(mem_b)
+            if b == 0:
+                nc.sync.dma_start(slot_sb[:], slot)
 
         picked_words = []
         picked_scales = []
@@ -72,9 +71,22 @@ def tile_picked_gmem_relu_e_kernel(tc, xT, mem, w1, w2, offs, slot, out):
         def pick(z):
             planes = keep.tile([P, PACK, S], BF16, name="planes%d" % z)
             for j in range(PACK):
-                nc.vector.tensor_copy(out=planes[:, j, :], in_=x_raw[z, j][:].indirect(offs_sb[:]))
+                if (z, j) == (1, 2):
+                    rounded = keep.tile([P, T], BF16, name="rounded")
+                    nc.scalar.activation(out=rounded[:], in_=x_raw[z, j][:], func=ACT.Copy)
+                    nc.scalar.activation(out=planes[:, j, :], in_=rounded[:].indirect(offs_sb[:]), func=ACT.Copy)
+                else:
+                    nc.vector.tensor_copy(out=planes[:, j, :], in_=x_raw[z, j][:].indirect(offs_sb[:]))
             grouped = keep.tile([P, S, PACK], BF16, name="x_grouped%d" % z, align_bytes=64)
-            interleave(nc, z == PASSES - 1, grouped[:], planes[:])
+            if z == 0:
+                for j in range(0, PACK, 2):
+                    nc.scalar.activation(
+                        out=grouped[:, :, j : j + 2],
+                        in_=planes[:, j : j + 2, :].rearrange("p t c -> p c t"),
+                        func=ACT.Copy,
+                    )
+            else:
+                interleave(nc, True, grouped[:], planes[:])
             return grouped
 
         def quantise_messages(z, grouped, tag):
@@ -86,31 +98,31 @@ def tile_picked_gmem_relu_e_kernel(tc, xT, mem, w1, w2, offs, slot, out):
             picked_words.append(words)
             picked_scales.append(scales)
 
-        w_words = [keep.tile([P, PASSES, 2 * P], U32, name="w_words%d" % b, align_bytes=64) for b in range(BLOCKS)]
-        w_scales = [keep.tile([P, PASSES, 2 * P], U8, name="w_scales%d" % b, align_bytes=64) for b in range(BLOCKS)]
+        w_words = {}
+        w_scales = {}
 
-        def quantise_weights(b, passes, tag):
-            grouped = keep.tile(
-                [P, len(passes), 2 * P, PACK], BF16, name="w_grouped%d_%d" % (b, passes[0]), tag=tag, align_bytes=64
-            )
-            for i, z in enumerate(passes):
-                for m in range(2):
-                    interleave(nc, False, grouped[:, i, m * P : (m + 1) * P, :], w_raw[b, z, m][:])
-            zs = slice(passes[0], passes[-1] + 1)
+        def quantise_weights(b, pieces, tag):
+            name = "%d_%d_%d" % (b, *pieces[0])
+            width = len(pieces) * P
+            grouped = keep.tile([P, width, PACK], BF16, name="w_grouped" + name, tag=tag, align_bytes=64)
+            words = keep.tile([P, width], U32, name="w_words" + name, align_bytes=64)
+            scales = keep.tile([P, width], U8, name="w_scales" + name, align_bytes=64)
+            for i, (m, z) in enumerate(pieces):
+                cols = slice(i * P, (i + 1) * P)
+                interleave(nc, False, grouped[:, cols, :], w_raw[b, z, m][:])
+                w_words[b, m, z] = words[:, cols]
+                w_scales[b, m, z] = scales[:, cols]
             nc.vector.quantize_mx(
-                out=w_words[b][:, zs, :].rearrange("p z c -> p (z c)").bitcast(FP8X4),
-                scales=w_scales[b][:, zs, :].rearrange("p z c -> p (z c)"),
-                in_=grouped[:].rearrange("p z c t -> p (z c t)"),
+                out=words[:].bitcast(FP8X4), scales=scales[:], in_=grouped[:].rearrange("p c t -> p (c t)")
             )
 
         acc = {(b, m): psum.tile([P, S], F32, name="acc%d_%d" % (b, m)) for b in range(BLOCKS) for m in range(2)}
 
         def product(b, m, z):
-            cols = slice(m * P, (m + 1) * P)
             nc.tensor.matmul_mx(
                 out=acc[b, m][:],
-                lhsT=w_words[b][:, z, cols].bitcast(FP8X4),
-                lhsT_scale=w_scales[b][:, z, cols],
+                lhsT=w_words[b, m, z].bitcast(FP8X4),
+                lhsT_scale=w_scales[b, m, z],
                 rhs=picked_words[z][:].bitcast(FP8X4),
                 rhs_scale=picked_scales[z][:],
                 start=(z == 0),
@@ -125,14 +137,17 @@ def tile_picked_gmem_relu_e_kernel(tc, xT, mem, w1, w2, offs, slot, out):
             nc.vector.tensor_tensor(step[:], dist[:, halves[h]], gate[:, halves[h]], ALU.mult)
             nc.vector.tensor_tensor(mem_sb[0][:].indirect(slot_halves[h]), step[:], old[:, halves[h]], ALU.add)
 
-        quantise_messages(0, pick(0), "picked_scales0")
+        grouped0 = pick(0)
         grouped1 = pick(1)
-        quantise_weights(0, [0], "hold_a")
+        quantise_messages(0, grouped0, "x_raw1_1")
+        quantise_weights(0, [(0, 0)], "hold_a")
         product(0, 0, 0)
+        quantise_weights(0, [(1, 0)], "w_grouped_a")
         product(0, 1, 0)
         quantise_messages(1, grouped1, "hold_a")
-        quantise_weights(0, [1], "hold_b")
+        quantise_weights(0, [(0, 1)], "w_grouped_b")
         product(0, 0, 1)
+        quantise_weights(0, [(1, 1)], "hold_b")
         product(0, 1, 1)
         gate0 = keep.tile([P, S], F32, name="gate0")
         nc.scalar.activation(out=gate0[:], in_=acc[0, 0][:], func=ACT.Sigmoid)
@@ -150,7 +165,7 @@ def tile_picked_gmem_relu_e_kernel(tc, xT, mem, w1, w2, offs, slot, out):
                 op1=ALU.subtract,
             )
         write_half(old, dist, gate0, 0, "step0")
-        quantise_weights(1, [0, 1], "hold_c")
+        quantise_weights(1, [(m, z) for m in range(2) for z in range(PASSES)], "hold_c")
         for m in range(2):
             for z in range(PASSES):
                 product(1, m, z)

@@ -19,15 +19,13 @@ PACK = 4
 K_PASS = P * PACK
 PASSES = K // K_PASS
 BLOCKS = N // P
+GATE, CAND = 0, 1
+HALF = S // 2
+PART_A, PART_B, PART_C = slice(0, 256), slice(256, 448), slice(448, 512)
 
 
-def interleave(nc, on_vector, grouped, raw):
-    dst = grouped.rearrange("p (c i) t -> p c t i", i=4)
-    src = raw.rearrange("p t (c i) -> p c t i", i=4)
-    if on_vector:
-        nc.vector.tensor_copy(out=dst, in_=src)
-    else:
-        nc.scalar.activation(out=dst, in_=src, func=ACT.Copy)
+def entries(list_sb, part):
+    return list_sb[:, part.start // 16 : part.stop // 16]
 
 
 def tile_picked_gmem_relu_e_kernel(tc, xT, mem, w1, w2, offs, slot, out):
@@ -51,145 +49,177 @@ def tile_picked_gmem_relu_e_kernel(tc, xT, mem, w1, w2, offs, slot, out):
         w_raw = {}
         mem_sb = []
         for b in range(BLOCKS):
-            pieces = [(z, m) for z in range(PASSES) for m in range(2)]
-            if b == 1:
-                pieces = [(z, m) for m in range(2) for z in range(PASSES)]
-            for z, m in pieces:
-                raw = keep.tile([P, PACK, P], F32, name="w_raw%d_%d_%d" % (b, z, m))
-                rows = (w2, w1)[m][z * K_PASS : (z + 1) * K_PASS, b * P : (b + 1) * P]
-                nc.sync.dma_start(out=raw[:], in_=rows.rearrange("(p j) c -> p j c", j=PACK))
-                w_raw[b, z, m] = raw
+            for m in (GATE, CAND):
+                for z in range(PASSES):
+                    raw = keep.tile([P, PACK, P], F32, name="w_raw%d_%d_%d" % (b, m, z))
+                    rows = (w2, w1)[m][z * K_PASS : (z + 1) * K_PASS, b * P : (b + 1) * P]
+                    nc.sync.dma_start(out=raw[:], in_=rows.rearrange("(p j) c -> p j c", j=PACK))
+                    w_raw[b, m, z] = raw
+            if b == 0:
+                nc.sync.dma_start(slot_sb[:], slot)
             mem_b = keep.tile([P, U], F32, name="mem%d" % b)
             nc.sync.dma_start(out=mem_b[:], in_=mem[b * P : (b + 1) * P, :])
             mem_sb.append(mem_b)
-            if b == 0:
-                nc.sync.dma_start(slot_sb[:], slot)
 
-        picked_words = []
-        picked_scales = []
+        warm = keep.tile([P, 1], F32, name="warm")
+        nc.scalar.activation(out=warm[:], in_=x_raw[0, 0][:, 0:1], func=ACT.Sigmoid)
 
-        def pick(z):
-            planes = keep.tile([P, PACK, S], BF16, name="planes%d" % z)
-            for j in range(PACK):
-                if (z, j) == (1, 2):
-                    rounded = keep.tile([P, T], BF16, name="rounded")
-                    nc.scalar.activation(out=rounded[:], in_=x_raw[z, j][:], func=ACT.Copy)
-                    nc.scalar.activation(out=planes[:, j, :], in_=rounded[:].indirect(offs_sb[:]), func=ACT.Copy)
-                else:
-                    nc.vector.tensor_copy(out=planes[:, j, :], in_=x_raw[z, j][:].indirect(offs_sb[:]))
-            grouped = keep.tile([P, S, PACK], BF16, name="x_grouped%d" % z, align_bytes=64)
-            if z == 0:
-                for j in range(0, PACK, 2):
-                    nc.scalar.activation(
-                        out=grouped[:, :, j : j + 2],
-                        in_=planes[:, j : j + 2, :].rearrange("p t c -> p c t"),
-                        func=ACT.Copy,
-                    )
-            else:
-                interleave(nc, True, grouped[:], planes[:])
-            return grouped
+        halves = [slice(0, S // 2), slice(S // 2, S)]
+        planes = [keep.tile([P, PACK, S], BF16, name="planes%d" % z) for z in range(PASSES)]
+        x_grouped = [keep.tile([P, S, PACK], BF16, name="x_grouped%d" % z, align_bytes=64) for z in range(PASSES)]
+        x_words = [keep.tile([P, S], U32, name="x_words%d" % z, align_bytes=64) for z in range(PASSES)]
+        x_scales = {}
 
-        def quantise_messages(z, grouped, tag):
-            words = keep.tile([P, S], U32, name="picked_words%d" % z, align_bytes=64)
-            scales = keep.tile([P, S], U8, name="picked_scales%d" % z, tag=tag, align_bytes=64)
-            nc.vector.quantize_mx(
-                out=words[:].bitcast(FP8X4), scales=scales[:], in_=grouped[:].rearrange("p c t -> p (c t)")
+        def gather_plane(z, j, part):
+            nc.vector.tensor_copy(out=planes[z][:, j, part], in_=x_raw[z, j][:].indirect(entries(offs_sb, part)))
+
+        def gather_plane_on_scalar(z, j):
+            rounded = keep.tile([P, T], BF16, name="rounded%d_%d" % (z, j))
+            nc.scalar.activation(out=rounded[:], in_=x_raw[z, j][:], func=ACT.Copy)
+            nc.scalar.activation(out=planes[z][:, j, :], in_=rounded[:].indirect(offs_sb[:]), func=ACT.Copy)
+
+        def weave(z, part):
+            nc.vector.tensor_copy(
+                out=x_grouped[z][:, part, :].rearrange("p (c i) t -> p c t i", i=4),
+                in_=planes[z][:, :, part].rearrange("p t (c i) -> p c t i", i=4),
             )
-            picked_words.append(words)
-            picked_scales.append(scales)
+
+        def quantise_messages(z, h, tag):
+            part = halves[h]
+            x_scales[z, h] = keep.tile([P, HALF], U8, name="x_scales%d_%d" % (z, h), tag=tag, align_bytes=64)
+            nc.vector.quantize_mx(
+                out=x_words[z][:, part].bitcast(FP8X4),
+                scales=x_scales[z, h][:],
+                in_=x_grouped[z][:, part, :].rearrange("p c t -> p (c t)"),
+            )
 
         w_words = {}
         w_scales = {}
 
-        def quantise_weights(b, pieces, tag):
-            name = "%d_%d_%d" % (b, *pieces[0])
-            width = len(pieces) * P
+        def group_weights(b, m, passes, tag):
+            name = "%d_%d_%d" % (b, m, passes[0])
+            width = len(passes) * P
             grouped = keep.tile([P, width, PACK], BF16, name="w_grouped" + name, tag=tag, align_bytes=64)
             words = keep.tile([P, width], U32, name="w_words" + name, align_bytes=64)
             scales = keep.tile([P, width], U8, name="w_scales" + name, align_bytes=64)
-            for i, (m, z) in enumerate(pieces):
+            for i, z in enumerate(passes):
                 cols = slice(i * P, (i + 1) * P)
-                interleave(nc, False, grouped[:, cols, :], w_raw[b, z, m][:])
+                nc.scalar.activation(
+                    out=grouped[:, cols, :].rearrange("p (c i) t -> p c t i", i=4),
+                    in_=w_raw[b, m, z][:].rearrange("p t (c i) -> p c t i", i=4),
+                    func=ACT.Copy,
+                )
                 w_words[b, m, z] = words[:, cols]
                 w_scales[b, m, z] = scales[:, cols]
+            return grouped, words, scales
+
+        def quantise_weights(grouped, words, scales):
             nc.vector.quantize_mx(
                 out=words[:].bitcast(FP8X4), scales=scales[:], in_=grouped[:].rearrange("p c t -> p (c t)")
             )
 
-        acc = {(b, m): psum.tile([P, S], F32, name="acc%d_%d" % (b, m)) for b in range(BLOCKS) for m in range(2)}
+        acc = {
+            (b, m, h): psum.tile([P, HALF], F32, name="acc%d_%d_%d" % (b, m, h))
+            for b in range(BLOCKS)
+            for m in range(2)
+            for h in range(2)
+        }
 
-        def product(b, m, z):
+        def product(b, m, z, h):
             nc.tensor.matmul_mx(
-                out=acc[b, m][:],
+                out=acc[b, m, h][:],
                 lhsT=w_words[b, m, z].bitcast(FP8X4),
                 lhsT_scale=w_scales[b, m, z],
-                rhs=picked_words[z][:].bitcast(FP8X4),
-                rhs_scale=picked_scales[z][:],
+                rhs=x_words[z][:, halves[h]].bitcast(FP8X4),
+                rhs_scale=x_scales[z, h][:],
                 start=(z == 0),
                 stop=(z == PASSES - 1),
             )
 
-        halves = [slice(h * S // 2, (h + 1) * S // 2) for h in range(2)]
-        slot_halves = [slot_sb[:, h * S // 32 : (h + 1) * S // 32] for h in range(2)]
-
-        def write_half(old, dist, gate, h, tag):
-            step = keep.tile([P, S // 2], F32, name="step%d" % h, tag=tag, align_bytes=64)
-            nc.vector.tensor_tensor(step[:], dist[:, halves[h]], gate[:, halves[h]], ALU.mult)
-            nc.vector.tensor_tensor(mem_sb[0][:].indirect(slot_halves[h]), step[:], old[:, halves[h]], ALU.add)
-
-        grouped0 = pick(0)
-        grouped1 = pick(1)
-        quantise_messages(0, grouped0, "x_raw1_1")
-        quantise_weights(0, [(0, 0)], "hold_a")
-        product(0, 0, 0)
-        quantise_weights(0, [(1, 0)], "w_grouped_a")
-        product(0, 1, 0)
-        quantise_messages(1, grouped1, "hold_a")
-        quantise_weights(0, [(0, 1)], "w_grouped_b")
-        product(0, 0, 1)
-        quantise_weights(0, [(1, 1)], "hold_b")
-        product(0, 1, 1)
-        gate0 = keep.tile([P, S], F32, name="gate0")
-        nc.scalar.activation(out=gate0[:], in_=acc[0, 0][:], func=ACT.Sigmoid)
-        old = keep.tile([P, S], F32, name="old", tag="hold_b", align_bytes=64)
-        dist = keep.tile([P, S], F32, name="dist")
+        whole = slice(0, S)
+        for j in range(PACK - 1):
+            gather_plane(0, j, whole)
+        for h in halves:
+            gather_plane(0, 3, h)
+        for h in halves:
+            weave(0, h)
         for h in range(2):
-            nc.vector.tensor_copy(out=old[:, halves[h]], in_=mem_sb[0][:].indirect(slot_halves[h]))
-        for h in range(2):
+            quantise_messages(0, h, "x_scales0_%d" % h)
+        gather_plane_on_scalar(1, 0)
+        gather_plane(1, 1, whole)
+        gather_plane_on_scalar(1, 2)
+        for h in halves:
+            gather_plane(1, 3, h)
+        for h in halves:
+            weave(1, h)
+        for z in range(PASSES):
+            quantise_weights(*group_weights(0, GATE, [z], "gate_w%d" % z))
+            quantise_messages(1, z, "gate_w%d" % z)
+        for z in range(PASSES):
+            for h in range(2):
+                product(0, GATE, z, h)
+
+        def gates(b):
+            rest = keep.tile([P, S], F32, name="rest%d" % b)
+            gate = [keep.tile([P, HALF], F32, name="gate%d_%d" % (b, h), align_bytes=64) for h in range(2)]
+            for h in range(2):
+                nc.scalar.activation(out=rest[:, halves[h]], in_=acc[b, GATE, h][:], func=ACT.Sigmoid, scale=-1.0)
+                nc.scalar.activation(out=gate[h][:], in_=acc[b, GATE, h][:], func=ACT.Sigmoid)
+            return rest, gate
+
+        def keep_old(dst, b, rest, part):
+            nc.vector.tensor_tensor(dst, mem_sb[b][:].indirect(entries(slot_sb, part)), rest[:, part], ALU.mult)
+
+        def make_fresh(dst, b, gate, part):
+            h, first = divmod(part.start, HALF)
+            cols = slice(first, first + part.stop - part.start)
             nc.vector.scalar_tensor_tensor(
-                out=dist[:, halves[h]],
-                in0=acc[0, 1][:, halves[h]],
-                scalar=0.0,
-                in1=old[:, halves[h]],
-                op0=ALU.max,
-                op1=ALU.subtract,
+                out=dst, in0=acc[b, CAND, h][:, cols], scalar=0.0, in1=gate[h][:, cols], op0=ALU.max, op1=ALU.mult
             )
-        write_half(old, dist, gate0, 0, "step0")
-        quantise_weights(1, [(m, z) for m in range(2) for z in range(PASSES)], "hold_c")
-        for m in range(2):
+
+        def put(b, kept, fresh, part):
+            nc.vector.tensor_tensor(mem_sb[b][:].indirect(entries(slot_sb, part)), kept, fresh, ALU.add)
+
+        for z in range(PASSES):
+            quantise_weights(*group_weights(0, CAND, [z], "cand_w%d" % z))
+        for h in range(2):
             for z in range(PASSES):
-                product(1, m, z)
-        write_half(old, dist, gate0, 1, "hold_c")
-        nc.sync.dma_start(out=out[0:P, :], in_=mem_sb[0][:])
+                product(0, CAND, z, h)
+        rest0, gate0 = gates(0)
 
-        rest1 = keep.tile([P, S], F32, name="rest1")
-        gate1 = keep.tile([P, S], F32, name="gate1")
-        nc.scalar.activation(out=rest1[:], in_=acc[1, 0][:], func=ACT.Sigmoid, scale=-1.0)
-        nc.scalar.activation(out=gate1[:], in_=acc[1, 0][:], func=ACT.Sigmoid)
-        kept = keep.tile([P, S], F32, name="kept")
-        fresh = keep.tile([P, S], F32, name="fresh")
-        nc.vector.tensor_tensor(kept[:], mem_sb[1][:].indirect(slot_sb[:]), rest1[:], ALU.mult)
+        kept0 = keep.tile([P, PART_B.stop], F32, name="kept0")
+        fresh0 = keep.tile([P, PART_A.stop], F32, name="fresh0")
+        keep_old(kept0[:, PART_A], 0, rest0, PART_A)
+        make_fresh(fresh0[:], 0, gate0, PART_A)
+        keep_old(kept0[:, PART_B], 0, rest0, PART_B)
+        put(0, kept0[:, PART_A], fresh0[:], PART_A)
+
+        gate_w = group_weights(1, GATE, [0, 1], "cand_w1")
+        cand_w = group_weights(1, CAND, [0, 1], "cand_w_b1")
+        quantise_weights(*gate_w)
         for h in range(2):
-            nc.vector.scalar_tensor_tensor(
-                out=fresh[:, halves[h]],
-                in0=acc[1, 1][:, halves[h]],
-                scalar=0.0,
-                in1=gate1[:, halves[h]],
-                op0=ALU.max,
-                op1=ALU.mult,
-            )
+            for z in range(PASSES):
+                product(1, GATE, z, h)
+        rest1, gate1 = gates(1)
+        late = keep.tile([P, S], F32, name="fresh0_late", tag="cand_w1", align_bytes=64)
+        make_fresh(late[:, PART_B], 0, gate0, PART_B)
+        make_fresh(late[:, PART_C], 0, gate0, PART_C)
+        put(0, kept0[:, PART_B], late[:, PART_B], PART_B)
+
+        quantise_weights(*cand_w)
         for h in range(2):
-            nc.vector.tensor_tensor(
-                mem_sb[1][:].indirect(slot_halves[h]), kept[:, halves[h]], fresh[:, halves[h]], ALU.add
-            )
+            for z in range(PASSES):
+                product(1, CAND, z, h)
+        kept1 = keep.tile([P, S], F32, name="kept1")
+        fresh1 = keep.tile([P, S], F32, name="fresh1")
+        for h in halves:
+            keep_old(kept1[:, h], 1, rest1, h)
+        for h in halves:
+            make_fresh(fresh1[:, h], 1, gate1, h)
+        kept0_late = keep.tile([P, S], F32, name="kept0_late", tag="gate1_0", align_bytes=64)
+        keep_old(kept0_late[:, PART_C], 0, rest0, PART_C)
+        put(1, kept1[:, halves[0]], fresh1[:, halves[0]], halves[0])
+        put(0, kept0_late[:, PART_C], late[:, PART_C], PART_C)
+        nc.sync.dma_start(out=out[0:P, :], in_=mem_sb[0][:])
+        put(1, kept1[:, halves[1]], fresh1[:, halves[1]], halves[1])
         nc.sync.dma_start(out=out[P : 2 * P, :], in_=mem_sb[1][:])

@@ -21,7 +21,7 @@ PASSES = K // K_PASS
 BLOCKS = N // P
 GATE, CAND = 0, 1
 HALF = S // 2
-PART_A, PART_B, PART_C = slice(0, 256), slice(256, 448), slice(448, 512)
+PART_A, PART_B, PART_C = slice(0, 256), slice(256, 384), slice(384, 512)
 
 
 def entries(list_sb, part):
@@ -51,7 +51,7 @@ def tile_picked_gmem_relu_e_kernel(tc, xT, mem, w1, w2, offs, slot, out):
         for b in range(BLOCKS):
             for m in (GATE, CAND):
                 for z in range(PASSES):
-                    raw = keep.tile([P, PACK, P], F32, name="w_raw%d_%d_%d" % (b, m, z))
+                    raw = keep.tile([P, PACK, P], F32, name="w_raw%d_%d_%d" % (b, m, z), align_bytes=64)
                     rows = (w2, w1)[m][z * K_PASS : (z + 1) * K_PASS, b * P : (b + 1) * P]
                     nc.sync.dma_start(out=raw[:], in_=rows.rearrange("(p j) c -> p j c", j=PACK))
                     w_raw[b, m, z] = raw
@@ -66,22 +66,18 @@ def tile_picked_gmem_relu_e_kernel(tc, xT, mem, w1, w2, offs, slot, out):
 
         halves = [slice(0, S // 2), slice(S // 2, S)]
         planes = [keep.tile([P, PACK, S], BF16, name="planes%d" % z) for z in range(PASSES)]
-        x_grouped = [keep.tile([P, S, PACK], BF16, name="x_grouped%d" % z, align_bytes=64) for z in range(PASSES)]
+        x_grouped = {}
         x_words = [keep.tile([P, S], U32, name="x_words%d" % z, align_bytes=64) for z in range(PASSES)]
         x_scales = {}
 
         def gather_plane(z, j, part):
             nc.vector.tensor_copy(out=planes[z][:, j, part], in_=x_raw[z, j][:].indirect(entries(offs_sb, part)))
 
-        def gather_plane_on_scalar(z, j):
-            rounded = keep.tile([P, T], BF16, name="rounded%d_%d" % (z, j))
-            nc.scalar.activation(out=rounded[:], in_=x_raw[z, j][:], func=ACT.Copy)
-            nc.scalar.activation(out=planes[z][:, j, :], in_=rounded[:].indirect(offs_sb[:]), func=ACT.Copy)
-
-        def weave(z, part):
+        def weave(z, h, tag):
+            x_grouped[z, h] = keep.tile([P, HALF, PACK], BF16, name="x_grouped%d_%d" % (z, h), tag=tag, align_bytes=64)
             nc.vector.tensor_copy(
-                out=x_grouped[z][:, part, :].rearrange("p (c i) t -> p c t i", i=4),
-                in_=planes[z][:, :, part].rearrange("p t (c i) -> p c t i", i=4),
+                out=x_grouped[z, h][:].rearrange("p (c i) t -> p c t i", i=4),
+                in_=planes[z][:, :, halves[h]].rearrange("p t (c i) -> p c t i", i=4),
             )
 
         def quantise_messages(z, h, tag):
@@ -90,7 +86,7 @@ def tile_picked_gmem_relu_e_kernel(tc, xT, mem, w1, w2, offs, slot, out):
             nc.vector.quantize_mx(
                 out=x_words[z][:, part].bitcast(FP8X4),
                 scales=x_scales[z, h][:],
-                in_=x_grouped[z][:, part, :].rearrange("p c t -> p (c t)"),
+                in_=x_grouped[z, h][:].rearrange("p c t -> p (c t)"),
             )
 
         w_words = {}
@@ -118,14 +114,11 @@ def tile_picked_gmem_relu_e_kernel(tc, xT, mem, w1, w2, offs, slot, out):
                 out=words[:].bitcast(FP8X4), scales=scales[:], in_=grouped[:].rearrange("p c t -> p (c t)")
             )
 
-        acc = {
-            (b, m, h): psum.tile([P, HALF], F32, name="acc%d_%d_%d" % (b, m, h))
-            for b in range(BLOCKS)
-            for m in range(2)
-            for h in range(2)
-        }
+        acc = {}
 
-        def product(b, m, z, h):
+        def product(b, m, z, h, tag):
+            if z == 0:
+                acc[b, m, h] = psum.tile([P, HALF], F32, name="acc%d_%d_%d" % (b, m, h), tag=tag)
             nc.tensor.matmul_mx(
                 out=acc[b, m, h][:],
                 lhsT=w_words[b, m, z].bitcast(FP8X4),
@@ -141,34 +134,53 @@ def tile_picked_gmem_relu_e_kernel(tc, xT, mem, w1, w2, offs, slot, out):
             gather_plane(0, j, whole)
         for h in halves:
             gather_plane(0, 3, h)
-        for h in halves:
-            weave(0, h)
+        for h in range(2):
+            weave(0, h, "x_grouped0_%d" % h)
         for h in range(2):
             quantise_messages(0, h, "x_scales0_%d" % h)
-        gather_plane_on_scalar(1, 0)
-        gather_plane(1, 1, whole)
-        gather_plane_on_scalar(1, 2)
+        rounded = [keep.tile([P, T], BF16, name="rounded%d" % j) for j in range(2)]
+        for j in range(2):
+            nc.scalar.activation(out=rounded[j][:], in_=x_raw[1, j][:], func=ACT.Copy)
+        for h in halves:
+            for j in range(2):
+                nc.scalar.activation(
+                    out=planes[1][:, j, h], in_=rounded[j][:].indirect(entries(offs_sb, h)), func=ACT.Copy
+                )
+        gather_plane(1, 2, whole)
         for h in halves:
             gather_plane(1, 3, h)
-        for h in halves:
-            weave(1, h)
+        weave(1, 0, "x_grouped1_0")
+        quantise_weights(*group_weights(0, GATE, [0], "gate_w0"))
+        quantise_messages(1, 0, "w_raw0_0_0")
+        quantise_weights(*group_weights(0, GATE, [1], "gate_w1"))
+        weave(1, 1, "w_raw0_0_1")
+        quantise_weights(*group_weights(0, CAND, [0], "cand_w0"))
+        quantise_messages(1, 1, "w_raw0_1_0")
+        quantise_weights(*group_weights(0, CAND, [1], "cand_w1"))
+        for h in range(2):
+            for z in range(PASSES):
+                product(0, GATE, z, h, "gate0_%d" % h)
         for z in range(PASSES):
-            quantise_weights(*group_weights(0, GATE, [z], "gate_w%d" % z))
-            quantise_messages(1, z, "gate_w%d" % z)
-        for z in range(PASSES):
-            for h in range(2):
-                product(0, GATE, z, h)
+            product(0, CAND, z, 0, "cand0")
 
-        def gates(b):
-            rest = keep.tile([P, S], F32, name="rest%d" % b)
-            gate = [keep.tile([P, HALF], F32, name="gate%d_%d" % (b, h), align_bytes=64) for h in range(2)]
+        def gates(b, parts):
+            rest = {}
+            gate = []
             for h in range(2):
-                nc.scalar.activation(out=rest[:, halves[h]], in_=acc[b, GATE, h][:], func=ACT.Sigmoid, scale=-1.0)
-                nc.scalar.activation(out=gate[h][:], in_=acc[b, GATE, h][:], func=ACT.Sigmoid)
+                for part in parts:
+                    if part.start // HALF == h:
+                        width = part.stop - part.start
+                        cols = slice(part.start % HALF, part.start % HALF + width)
+                        tile = keep.tile([P, width], F32, name="rest%d_%d" % (b, part.start), align_bytes=64)
+                        nc.scalar.activation(out=tile[:], in_=acc[b, GATE, h][:, cols], func=ACT.Sigmoid, scale=-1.0)
+                        rest[part.start] = tile
+                tile = keep.tile([P, HALF], F32, name="gate%d_%d" % (b, h), align_bytes=64)
+                nc.scalar.activation(out=tile[:], in_=acc[b, GATE, h][:], func=ACT.Sigmoid)
+                gate.append(tile)
             return rest, gate
 
         def keep_old(dst, b, rest, part):
-            nc.vector.tensor_tensor(dst, mem_sb[b][:].indirect(entries(slot_sb, part)), rest[:, part], ALU.mult)
+            nc.vector.tensor_tensor(dst, mem_sb[b][:].indirect(entries(slot_sb, part)), rest[part.start][:], ALU.mult)
 
         def make_fresh(dst, b, gate, part):
             h, first = divmod(part.start, HALF)
@@ -180,28 +192,25 @@ def tile_picked_gmem_relu_e_kernel(tc, xT, mem, w1, w2, offs, slot, out):
         def put(b, kept, fresh, part):
             nc.vector.tensor_tensor(mem_sb[b][:].indirect(entries(slot_sb, part)), kept, fresh, ALU.add)
 
-        for z in range(PASSES):
-            quantise_weights(*group_weights(0, CAND, [z], "cand_w%d" % z))
-        for h in range(2):
-            for z in range(PASSES):
-                product(0, CAND, z, h)
-        rest0, gate0 = gates(0)
+        rest0, gate0 = gates(0, [PART_A, PART_B, PART_C])
 
         kept0 = keep.tile([P, PART_B.stop], F32, name="kept0")
-        fresh0 = keep.tile([P, PART_A.stop], F32, name="fresh0")
         keep_old(kept0[:, PART_A], 0, rest0, PART_A)
+        fresh0 = keep.tile([P, PART_A.stop], F32, name="fresh0", tag="rest0_0", align_bytes=64)
         make_fresh(fresh0[:], 0, gate0, PART_A)
+        for z in range(PASSES):
+            product(0, CAND, z, 1, "cand0")
         keep_old(kept0[:, PART_B], 0, rest0, PART_B)
         put(0, kept0[:, PART_A], fresh0[:], PART_A)
 
-        gate_w = group_weights(1, GATE, [0, 1], "cand_w1")
+        gate_w = group_weights(1, GATE, [0, 1], "rest0_256")
         cand_w = group_weights(1, CAND, [0, 1], "cand_w_b1")
         quantise_weights(*gate_w)
         for h in range(2):
             for z in range(PASSES):
-                product(1, GATE, z, h)
-        rest1, gate1 = gates(1)
-        late = keep.tile([P, S], F32, name="fresh0_late", tag="cand_w1", align_bytes=64)
+                product(1, GATE, z, h, "gate1_%d" % h)
+        rest1, gate1 = gates(1, halves)
+        late = keep.tile([P, S], F32, name="fresh0_late", tag="w_raw1_0_1", align_bytes=64)
         make_fresh(late[:, PART_B], 0, gate0, PART_B)
         make_fresh(late[:, PART_C], 0, gate0, PART_C)
         put(0, kept0[:, PART_B], late[:, PART_B], PART_B)
@@ -209,17 +218,17 @@ def tile_picked_gmem_relu_e_kernel(tc, xT, mem, w1, w2, offs, slot, out):
         quantise_weights(*cand_w)
         for h in range(2):
             for z in range(PASSES):
-                product(1, CAND, z, h)
+                product(1, CAND, z, h, "cand1_%d" % h)
         kept1 = keep.tile([P, S], F32, name="kept1")
         fresh1 = keep.tile([P, S], F32, name="fresh1")
-        for h in halves:
-            keep_old(kept1[:, h], 1, rest1, h)
-        for h in halves:
-            make_fresh(fresh1[:, h], 1, gate1, h)
-        kept0_late = keep.tile([P, S], F32, name="kept0_late", tag="gate1_0", align_bytes=64)
+        kept0_late = keep.tile([P, S], F32, name="kept0_late", tag="w_raw1_1_1", align_bytes=64)
         keep_old(kept0_late[:, PART_C], 0, rest0, PART_C)
-        put(1, kept1[:, halves[0]], fresh1[:, halves[0]], halves[0])
+        keep_old(kept1[:, halves[0]], 1, rest1, halves[0])
         put(0, kept0_late[:, PART_C], late[:, PART_C], PART_C)
         nc.sync.dma_start(out=out[0:P, :], in_=mem_sb[0][:])
-        put(1, kept1[:, halves[1]], fresh1[:, halves[1]], halves[1])
+        keep_old(kept1[:, halves[1]], 1, rest1, halves[1])
+        for h in halves:
+            make_fresh(fresh1[:, h], 1, gate1, h)
+        for h in halves:
+            put(1, kept1[:, h], fresh1[:, h], h)
         nc.sync.dma_start(out=out[P : 2 * P, :], in_=mem_sb[1][:])

@@ -22,6 +22,7 @@ BLOCKS = N // P
 GATE, CAND = 0, 1
 HALF = S // 2
 PART_A, PART_B, PART_C = slice(0, 256), slice(256, 384), slice(384, 512)
+FIRST, SECOND = slice(0, 128), slice(128, 256)
 
 
 def entries(list_sb, part):
@@ -192,10 +193,11 @@ def tile_picked_gmem_relu_e_kernel(tc, xT, mem, w1, w2, offs, slot, out):
         def put(b, kept, fresh, part):
             nc.vector.tensor_tensor(mem_sb[b][:].indirect(entries(slot_sb, part)), kept, fresh, ALU.add)
 
-        rest0, gate0 = gates(0, [PART_A, PART_B, PART_C])
+        rest0, gate0 = gates(0, [FIRST, SECOND, PART_B, PART_C])
 
         kept0 = keep.tile([P, PART_B.stop], F32, name="kept0")
-        keep_old(kept0[:, PART_A], 0, rest0, PART_A)
+        for part in (FIRST, SECOND):
+            keep_old(kept0[:, part], 0, rest0, part)
         fresh0 = keep.tile([P, PART_A.stop], F32, name="fresh0", tag="rest0_0", align_bytes=64)
         make_fresh(fresh0[:], 0, gate0, PART_A)
         for z in range(PASSES):
@@ -229,6 +231,5 @@ def tile_picked_gmem_relu_e_kernel(tc, xT, mem, w1, w2, offs, slot, out):
         keep_old(kept1[:, halves[1]], 1, rest1, halves[1])
         for h in halves:
             make_fresh(fresh1[:, h], 1, gate1, h)
-        for h in halves:
-            put(1, kept1[:, h], fresh1[:, h], h)
+        put(1, kept1[:], fresh1[:], whole)
         nc.sync.dma_start(out=out[P : 2 * P, :], in_=mem_sb[1][:])

@@ -8,6 +8,7 @@ FLOPS = 2 * 2 * K * N * S
 F32 = mybir.dt.float32
 BF16 = mybir.dt.bfloat16
 U32 = mybir.dt.uint32
+I32 = mybir.dt.int32
 U16 = mybir.dt.uint16
 U8 = mybir.dt.uint8
 FP8X4 = mybir.dt.float8_e4m3fn_x4
@@ -21,6 +22,7 @@ PASSES = K // K_PASS
 BLOCKS = N // P
 GATE, CAND = 0, 1
 HALF = S // 2
+QUARTER = S // 4
 PART_A, PART_B, PART_C = slice(0, 256), slice(256, 384), slice(384, 512)
 FIRST, SECOND = slice(0, 128), slice(128, 256)
 
@@ -66,19 +68,25 @@ def tile_picked_gmem_relu_e_kernel(tc, xT, mem, w1, w2, offs, slot, out):
         nc.scalar.activation(out=warm[:], in_=x_raw[0, 0][:, 0:1], func=ACT.Sigmoid)
 
         halves = [slice(0, S // 2), slice(S // 2, S)]
-        planes = [keep.tile([P, PACK, S], BF16, name="planes%d" % z) for z in range(PASSES)]
+        pairs = [keep.tile([P, 4, 2, QUARTER, 2], BF16, name="pairs%d" % z) for z in range(PASSES)]
         x_grouped = {}
         x_words = [keep.tile([P, S], U32, name="x_words%d" % z, align_bytes=64) for z in range(PASSES)]
         x_scales = {}
 
+        def place(z, j, part):
+            return pairs[z][:, part.start // QUARTER : part.stop // QUARTER, j // 2, :, j % 2]
+
         def gather_plane(z, j, part):
-            nc.vector.tensor_copy(out=planes[z][:, j, part], in_=x_raw[z, j][:].indirect(entries(offs_sb, part)))
+            nc.vector.tensor_copy(out=place(z, j, part), in_=x_raw[z, j][:].indirect(entries(offs_sb, part)))
 
         def weave(z, h, tag):
             x_grouped[z, h] = keep.tile([P, HALF, PACK], BF16, name="x_grouped%d_%d" % (z, h), tag=tag, align_bytes=64)
             nc.vector.tensor_copy(
-                out=x_grouped[z, h][:].rearrange("p (c i) t -> p c t i", i=4),
-                in_=planes[z][:, :, halves[h]].rearrange("p t (c i) -> p c t i", i=4),
+                out=x_grouped[z, h][:].rearrange("p c t -> p (c t)").bitcast(I32).rearrange("p (q c u) -> p q c u", q=2, u=2),
+                in_=pairs[z][:, 2 * h : 2 * h + 2]
+                .rearrange("p q u c e -> p (q u c e)")
+                .bitcast(I32)
+                .rearrange("p (q u c) -> p q c u", q=2, u=2),
             )
 
         def quantise_messages(z, h, tag):
@@ -142,22 +150,23 @@ def tile_picked_gmem_relu_e_kernel(tc, xT, mem, w1, w2, offs, slot, out):
         rounded = [keep.tile([P, T], BF16, name="rounded%d" % j) for j in range(2)]
         for j in range(2):
             nc.scalar.activation(out=rounded[j][:], in_=x_raw[1, j][:], func=ACT.Copy)
-        for h in halves:
-            for j in range(2):
-                nc.scalar.activation(
-                    out=planes[1][:, j, h], in_=rounded[j][:].indirect(entries(offs_sb, h)), func=ACT.Copy
-                )
+        by_scalar, by_vector = slice(0, 3 * QUARTER), slice(3 * QUARTER, S)
+        for j in range(2):
+            nc.scalar.activation(
+                out=place(1, j, by_scalar), in_=rounded[j][:].indirect(entries(offs_sb, by_scalar)), func=ACT.Copy
+            )
+            gather_plane(1, j, by_vector)
         gather_plane(1, 2, whole)
         for h in halves:
             gather_plane(1, 3, h)
-        weave(1, 0, "x_grouped1_0")
+        for h in range(2):
+            weave(1, h, "x_grouped1_%d" % h)
         quantise_weights(*group_weights(0, GATE, [0], "gate_w0"))
         quantise_messages(1, 0, "w_raw0_0_0")
         quantise_weights(*group_weights(0, GATE, [1], "gate_w1"))
-        weave(1, 1, "w_raw0_0_1")
-        quantise_weights(*group_weights(0, CAND, [0], "cand_w0"))
-        quantise_messages(1, 1, "w_raw0_1_0")
-        quantise_weights(*group_weights(0, CAND, [1], "cand_w1"))
+        quantise_messages(1, 1, "w_raw0_0_1")
+        for z in range(PASSES):
+            quantise_weights(*group_weights(0, CAND, [z], "cand_w%d" % z))
         for h in range(2):
             for z in range(PASSES):
                 product(0, GATE, z, h, "gate0_%d" % h)

@@ -23,8 +23,8 @@ BLOCKS = N // P
 GATE, CAND = 0, 1
 HALF = S // 2
 QUARTER = S // 4
-PART_A, PART_B, PART_C = slice(0, 256), slice(256, 384), slice(384, 512)
-FIRST, SECOND = slice(0, 128), slice(128, 256)
+PART_A, PART_B, PART_C, PART_D = slice(0, 160), slice(160, 352), slice(352, 448), slice(448, 512)
+B_EARLY, B_LATE = slice(160, 256), slice(256, 352)
 
 
 def entries(list_sb, part):
@@ -43,10 +43,12 @@ def tile_picked_gmem_relu_e_kernel(tc, xT, mem, w1, w2, offs, slot, out):
         x_raw = {}
         for z in range(PASSES):
             rows = xT[z * K_PASS : (z + 1) * K_PASS, :].rearrange("(p j) t -> p j t", j=PACK)
-            for j in range(PACK):
-                raw = keep.tile([P, T], F32, name="x_raw%d_%d" % (z, j), align_bytes=64)
-                nc.sync.dma_start(out=raw[:], in_=rows[:, j, :])
-                x_raw[z, j] = raw
+            step = 1
+            for j in range(0, PACK, step):
+                raw = keep.tile([P, step * T], F32, name="x_raw%d_%d" % (z, j), align_bytes=64)
+                nc.sync.dma_start(out=raw[:], in_=rows[:, j : j + step, :].rearrange("p j t -> p (j t)"))
+                for i in range(step):
+                    x_raw[z, j + i] = raw[:, i * T : (i + 1) * T]
                 if (z, j) == (0, 0):
                     nc.sync.dma_start(offs_sb[:], offs)
         w_raw = {}
@@ -54,10 +56,14 @@ def tile_picked_gmem_relu_e_kernel(tc, xT, mem, w1, w2, offs, slot, out):
         for b in range(BLOCKS):
             for m in (GATE, CAND):
                 for z in range(PASSES):
-                    raw = keep.tile([P, PACK, P], F32, name="w_raw%d_%d_%d" % (b, m, z), align_bytes=64)
+                    lead = HALF if (b, m, z) == (1, GATE, 1) else 0
+                    tile = keep.tile([P, lead + PACK * P], F32, name="w_raw%d_%d_%d" % (b, m, z), align_bytes=64)
+                    raw = tile[:, lead:].rearrange("p (j c) -> p j c", j=PACK)
                     rows = (w2, w1)[m][z * K_PASS : (z + 1) * K_PASS, b * P : (b + 1) * P]
-                    nc.sync.dma_start(out=raw[:], in_=rows.rearrange("(p j) c -> p j c", j=PACK))
+                    nc.sync.dma_start(out=raw, in_=rows.rearrange("(p j) c -> p j c", j=PACK))
                     w_raw[b, m, z] = raw
+                    if lead:
+                        fresh_ab = tile
             if b == 0:
                 nc.sync.dma_start(slot_sb[:], slot)
             mem_b = keep.tile([P, U], F32, name="mem%d" % b)
@@ -77,7 +83,7 @@ def tile_picked_gmem_relu_e_kernel(tc, xT, mem, w1, w2, offs, slot, out):
             return pairs[z][:, part.start // QUARTER : part.stop // QUARTER, j // 2, :, j % 2]
 
         def gather_plane(z, j, part):
-            nc.vector.tensor_copy(out=place(z, j, part), in_=x_raw[z, j][:].indirect(entries(offs_sb, part)))
+            nc.vector.tensor_copy(out=place(z, j, part), in_=x_raw[z, j].indirect(entries(offs_sb, part)))
 
         def weave(z, h, tag):
             x_grouped[z, h] = keep.tile([P, HALF, PACK], BF16, name="x_grouped%d_%d" % (z, h), tag=tag, align_bytes=64)
@@ -101,7 +107,7 @@ def tile_picked_gmem_relu_e_kernel(tc, xT, mem, w1, w2, offs, slot, out):
         w_words = {}
         w_scales = {}
 
-        def group_weights(b, m, passes, tag):
+        def group_weights(b, m, passes, tag, on_vector=False):
             name = "%d_%d_%d" % (b, m, passes[0])
             width = len(passes) * P
             grouped = keep.tile([P, width, PACK], BF16, name="w_grouped" + name, tag=tag, align_bytes=64)
@@ -109,11 +115,12 @@ def tile_picked_gmem_relu_e_kernel(tc, xT, mem, w1, w2, offs, slot, out):
             scales = keep.tile([P, width], U8, name="w_scales" + name, align_bytes=64)
             for i, z in enumerate(passes):
                 cols = slice(i * P, (i + 1) * P)
-                nc.scalar.activation(
-                    out=grouped[:, cols, :].rearrange("p (c i) t -> p c t i", i=4),
-                    in_=w_raw[b, m, z][:].rearrange("p t (c i) -> p c t i", i=4),
-                    func=ACT.Copy,
-                )
+                dst = grouped[:, cols, :].rearrange("p (c i) t -> p c t i", i=4)
+                src = w_raw[b, m, z].rearrange("p t (c i) -> p c t i", i=4)
+                if on_vector:
+                    nc.vector.tensor_copy(out=dst, in_=src)
+                else:
+                    nc.scalar.activation(out=dst, in_=src, func=ACT.Copy)
                 w_words[b, m, z] = words[:, cols]
                 w_scales[b, m, z] = scales[:, cols]
             return grouped, words, scales
@@ -149,7 +156,7 @@ def tile_picked_gmem_relu_e_kernel(tc, xT, mem, w1, w2, offs, slot, out):
             quantise_messages(0, h, "x_scales0_%d" % h)
         rounded = [keep.tile([P, T], BF16, name="rounded%d" % j) for j in range(2)]
         for j in range(2):
-            nc.scalar.activation(out=rounded[j][:], in_=x_raw[1, j][:], func=ACT.Copy)
+            nc.scalar.activation(out=rounded[j][:], in_=x_raw[1, j], func=ACT.Copy)
         by_scalar, by_vector = slice(0, 3 * QUARTER), slice(3 * QUARTER, S)
         for j in range(2):
             nc.scalar.activation(
@@ -159,86 +166,95 @@ def tile_picked_gmem_relu_e_kernel(tc, xT, mem, w1, w2, offs, slot, out):
         gather_plane(1, 2, whole)
         for h in halves:
             gather_plane(1, 3, h)
-        for h in range(2):
-            weave(1, h, "x_grouped1_%d" % h)
+        weave(1, 0, "x_grouped1_0")
         quantise_weights(*group_weights(0, GATE, [0], "gate_w0"))
         quantise_messages(1, 0, "w_raw0_0_0")
         quantise_weights(*group_weights(0, GATE, [1], "gate_w1"))
-        quantise_messages(1, 1, "w_raw0_0_1")
-        for z in range(PASSES):
-            quantise_weights(*group_weights(0, CAND, [z], "cand_w%d" % z))
+        weave(1, 1, "w_raw0_0_1")
+        quantise_messages(1, 1, "x_scales1_1")
+        cand_w0 = [group_weights(0, CAND, [z], "cand_w%d" % z, on_vector=(z == PASSES - 1)) for z in range(PASSES)]
+        for tiles in cand_w0:
+            quantise_weights(*tiles)
         for h in range(2):
             for z in range(PASSES):
                 product(0, GATE, z, h, "gate0_%d" % h)
         for z in range(PASSES):
-            product(0, CAND, z, 0, "cand0")
-
-        def gates(b, parts):
-            rest = {}
-            gate = []
             for h in range(2):
-                for part in parts:
-                    if part.start // HALF == h:
-                        width = part.stop - part.start
-                        cols = slice(part.start % HALF, part.start % HALF + width)
-                        tile = keep.tile([P, width], F32, name="rest%d_%d" % (b, part.start), align_bytes=64)
-                        nc.scalar.activation(out=tile[:], in_=acc[b, GATE, h][:, cols], func=ACT.Sigmoid, scale=-1.0)
-                        rest[part.start] = tile
-                tile = keep.tile([P, HALF], F32, name="gate%d_%d" % (b, h), align_bytes=64)
-                nc.scalar.activation(out=tile[:], in_=acc[b, GATE, h][:], func=ACT.Sigmoid)
-                gate.append(tile)
-            return rest, gate
+                product(0, CAND, z, h, "cand0_%d" % h)
+
+        def sigmoids(b, parts, scale, name, given):
+            tiles = {}
+            for part in parts:
+                h, first = divmod(part.start, HALF)
+                width = part.stop - part.start
+                if part.start in given:
+                    dst = given[part.start]
+                else:
+                    tile = keep.tile([P, width], F32, name="%s%d_%d" % (name, b, part.start), align_bytes=64)
+                    dst = tile[:]
+                nc.scalar.activation(
+                    out=dst, in_=acc[b, GATE, h][:, first : first + width], func=ACT.Sigmoid, scale=scale
+                )
+                tiles[part.start] = dst
+            return tiles
 
         def keep_old(dst, b, rest, part):
-            nc.vector.tensor_tensor(dst, mem_sb[b][:].indirect(entries(slot_sb, part)), rest[part.start][:], ALU.mult)
+            nc.vector.tensor_tensor(dst, mem_sb[b][:].indirect(entries(slot_sb, part)), rest[part.start], ALU.mult)
 
         def make_fresh(dst, b, gate, part):
             h, first = divmod(part.start, HALF)
             cols = slice(first, first + part.stop - part.start)
             nc.vector.scalar_tensor_tensor(
-                out=dst, in0=acc[b, CAND, h][:, cols], scalar=0.0, in1=gate[h][:, cols], op0=ALU.max, op1=ALU.mult
+                out=dst,
+                in0=acc[b, CAND, h][:, cols],
+                scalar=0.0,
+                in1=gate[h * HALF][:, cols],
+                op0=ALU.max,
+                op1=ALU.mult,
             )
 
         def put(b, kept, fresh, part):
             nc.vector.tensor_tensor(mem_sb[b][:].indirect(entries(slot_sb, part)), kept, fresh, ALU.add)
 
-        rest0, gate0 = gates(0, [FIRST, SECOND, PART_B, PART_C])
+        third, fourth = slice(256, 320), slice(320, 512)
+        rest0 = sigmoids(0, [halves[0], third, fourth], -1.0, "rest", {0: fresh_ab[:, halves[0]]})
+        gate0 = sigmoids(0, halves, 1.0, "gate", {})
 
-        kept0 = keep.tile([P, PART_B.stop], F32, name="kept0")
-        for part in (FIRST, SECOND):
+        kept0 = keep.tile([P, S], F32, name="kept0")
+        for part in (halves[0], third, fourth):
             keep_old(kept0[:, part], 0, rest0, part)
-        fresh0 = keep.tile([P, PART_A.stop], F32, name="fresh0", tag="rest0_0", align_bytes=64)
-        make_fresh(fresh0[:], 0, gate0, PART_A)
-        for z in range(PASSES):
-            product(0, CAND, z, 1, "cand0")
-        keep_old(kept0[:, PART_B], 0, rest0, PART_B)
-        put(0, kept0[:, PART_A], fresh0[:], PART_A)
+        make_fresh(fresh_ab[:, PART_A], 0, gate0, PART_A)
+        make_fresh(fresh_ab[:, B_EARLY], 0, gate0, B_EARLY)
+        put(0, kept0[:, PART_A], fresh_ab[:, PART_A], PART_A)
 
         gate_w = group_weights(1, GATE, [0, 1], "rest0_256")
-        cand_w = group_weights(1, CAND, [0, 1], "cand_w_b1")
+        cand_w = [group_weights(1, CAND, [z], "cand_w_b1_%d" % z) for z in range(PASSES)]
+        make_fresh(fresh_ab[:, B_LATE], 0, gate0, B_LATE)
         quantise_weights(*gate_w)
         for h in range(2):
             for z in range(PASSES):
                 product(1, GATE, z, h, "gate1_%d" % h)
-        rest1, gate1 = gates(1, halves)
-        late = keep.tile([P, S], F32, name="fresh0_late", tag="w_raw1_0_1", align_bytes=64)
-        make_fresh(late[:, PART_B], 0, gate0, PART_B)
-        make_fresh(late[:, PART_C], 0, gate0, PART_C)
-        put(0, kept0[:, PART_B], late[:, PART_B], PART_B)
+        rest1 = sigmoids(1, halves, -1.0, "rest", {})
+        gate1 = sigmoids(1, halves, 1.0, "gate", {})
+        put(0, kept0[:, PART_B], fresh_ab[:, PART_B], PART_B)
 
-        quantise_weights(*cand_w)
-        for h in range(2):
-            for z in range(PASSES):
+        fresh_c = keep.tile([P, PART_C.stop - PART_C.start], F32, name="fresh_c", tag="w_raw1_1_0", align_bytes=64)
+        make_fresh(fresh_c[:], 0, gate0, PART_C)
+        quantise_weights(*cand_w[0])
+        put(0, kept0[:, PART_C], fresh_c[:], PART_C)
+        quantise_weights(*cand_w[1])
+        for z in range(PASSES):
+            for h in range(2):
                 product(1, CAND, z, h, "cand1_%d" % h)
         kept1 = keep.tile([P, S], F32, name="kept1")
         fresh1 = keep.tile([P, S], F32, name="fresh1")
-        kept0_late = keep.tile([P, S], F32, name="kept0_late", tag="w_raw1_1_1", align_bytes=64)
-        keep_old(kept0_late[:, PART_C], 0, rest0, PART_C)
-        keep_old(kept1[:, halves[0]], 1, rest1, halves[0])
-        put(0, kept0_late[:, PART_C], late[:, PART_C], PART_C)
-        nc.sync.dma_start(out=out[0:P, :], in_=mem_sb[0][:])
-        keep_old(kept1[:, halves[1]], 1, rest1, halves[1])
         for h in halves:
-            make_fresh(fresh1[:, h], 1, gate1, h)
+            keep_old(kept1[:, h], 1, rest1, h)
+        make_fresh(fresh1[:, halves[0]], 1, gate1, halves[0])
+        fresh_d = keep.tile([P, PART_D.stop - PART_D.start], F32, name="fresh_d", tag="w_words1_1_1", align_bytes=64)
+        make_fresh(fresh_d[:], 0, gate0, PART_D)
+        make_fresh(fresh1[:, halves[1]], 1, gate1, halves[1])
+        put(0, kept0[:, PART_D], fresh_d[:], PART_D)
+        nc.sync.dma_start(out=out[0:P, :], in_=mem_sb[0][:])
         put(1, kept1[:], fresh1[:], whole)
         nc.sync.dma_start(out=out[P : 2 * P, :], in_=mem_sb[1][:])

@@ -23,8 +23,6 @@ BLOCKS = N // P
 GATE, CAND = 0, 1
 HALF = S // 2
 QUARTER = S // 4
-PART_A, PART_B, PART_C, PART_D = slice(0, 160), slice(160, 352), slice(352, 448), slice(448, 512)
-B_EARLY, B_LATE = slice(160, 256), slice(256, 352)
 
 
 def entries(list_sb, part):
@@ -43,29 +41,23 @@ def tile_picked_gmem_relu_e_kernel(tc, xT, mem, w1, w2, offs, slot, out):
         x_raw = {}
         for z in range(PASSES):
             rows = xT[z * K_PASS : (z + 1) * K_PASS, :].rearrange("(p j) t -> p j t", j=PACK)
-            step = 1
-            for j in range(0, PACK, step):
-                raw = keep.tile([P, step * T], F32, name="x_raw%d_%d" % (z, j), align_bytes=64)
-                nc.sync.dma_start(out=raw[:], in_=rows[:, j : j + step, :].rearrange("p j t -> p (j t)"))
-                for i in range(step):
-                    x_raw[z, j + i] = raw[:, i * T : (i + 1) * T]
+            for j in range(PACK):
+                raw = keep.tile([P, T], F32, name="x_raw%d_%d" % (z, j), align_bytes=64)
+                nc.sync.dma_start(out=raw[:], in_=rows[:, j, :])
+                x_raw[z, j] = raw[:]
                 if (z, j) == (0, 0):
                     nc.sync.dma_start(offs_sb[:], offs)
         w_raw = {}
+        for m in (GATE, CAND):
+            for z in range(PASSES):
+                raw = keep.tile([P, PACK * N], F32, name="w_raw%d_%d" % (m, z), align_bytes=64)
+                rows = (w2, w1)[m][z * K_PASS : (z + 1) * K_PASS, :]
+                nc.sync.dma_start(out=raw[:], in_=rows.rearrange("(p j) c -> p (j c)", j=PACK))
+                w_raw[m, z] = raw[:].rearrange("p (j c) -> p j c", j=PACK)
+            if m == GATE:
+                nc.sync.dma_start(slot_sb[:], slot)
         mem_sb = []
         for b in range(BLOCKS):
-            for m in (GATE, CAND):
-                for z in range(PASSES):
-                    lead = HALF if (b, m, z) == (1, GATE, 1) else 0
-                    tile = keep.tile([P, lead + PACK * P], F32, name="w_raw%d_%d_%d" % (b, m, z), align_bytes=64)
-                    raw = tile[:, lead:].rearrange("p (j c) -> p j c", j=PACK)
-                    rows = (w2, w1)[m][z * K_PASS : (z + 1) * K_PASS, b * P : (b + 1) * P]
-                    nc.sync.dma_start(out=raw, in_=rows.rearrange("(p j) c -> p j c", j=PACK))
-                    w_raw[b, m, z] = raw
-                    if lead:
-                        fresh_ab = tile
-            if b == 0:
-                nc.sync.dma_start(slot_sb[:], slot)
             mem_b = keep.tile([P, U], F32, name="mem%d" % b)
             nc.sync.dma_start(out=mem_b[:], in_=mem[b * P : (b + 1) * P, :])
             mem_sb.append(mem_b)
@@ -73,11 +65,13 @@ def tile_picked_gmem_relu_e_kernel(tc, xT, mem, w1, w2, offs, slot, out):
         warm = keep.tile([P, 1], F32, name="warm")
         nc.scalar.activation(out=warm[:], in_=x_raw[0, 0][:, 0:1], func=ACT.Sigmoid)
 
-        halves = [slice(0, S // 2), slice(S // 2, S)]
+        whole = slice(0, S)
+        halves = [slice(0, HALF), slice(HALF, S)]
         pairs = [keep.tile([P, 4, 2, QUARTER, 2], BF16, name="pairs%d" % z) for z in range(PASSES)]
         x_grouped = {}
         x_words = [keep.tile([P, S], U32, name="x_words%d" % z, align_bytes=64) for z in range(PASSES)]
-        x_scales = {}
+        scales0 = keep.tile([P, S], U8, name="x_scales0", align_bytes=64)
+        x_scales = {(0, 0, HALF): scales0[:, :HALF], (0, HALF, S): scales0[:, HALF:], (0, 0, S): scales0[:]}
 
         def place(z, j, part):
             return pairs[z][:, part.start // QUARTER : part.stop // QUARTER, j // 2, :, j % 2]
@@ -85,8 +79,8 @@ def tile_picked_gmem_relu_e_kernel(tc, xT, mem, w1, w2, offs, slot, out):
         def gather_plane(z, j, part):
             nc.vector.tensor_copy(out=place(z, j, part), in_=x_raw[z, j].indirect(entries(offs_sb, part)))
 
-        def weave(z, h, tag):
-            x_grouped[z, h] = keep.tile([P, HALF, PACK], BF16, name="x_grouped%d_%d" % (z, h), tag=tag, align_bytes=64)
+        def weave(z, h):
+            x_grouped[z, h] = keep.tile([P, HALF, PACK], BF16, name="x_grouped%d_%d" % (z, h), align_bytes=64)
             nc.vector.tensor_copy(
                 out=x_grouped[z, h][:].rearrange("p c t -> p (c t)").bitcast(I32).rearrange("p (q c u) -> p q c u", q=2, u=2),
                 in_=pairs[z][:, 2 * h : 2 * h + 2]
@@ -95,70 +89,81 @@ def tile_picked_gmem_relu_e_kernel(tc, xT, mem, w1, w2, offs, slot, out):
                 .rearrange("p (q u c) -> p q c u", q=2, u=2),
             )
 
-        def quantise_messages(z, h, tag):
+        def quantise_messages(z, h):
             part = halves[h]
-            x_scales[z, h] = keep.tile([P, HALF], U8, name="x_scales%d_%d" % (z, h), tag=tag, align_bytes=64)
+            if z == 1:
+                tile = keep.tile([P, HALF], U8, name="x_scales1_%d" % h, tag="w_grouped0_0_%d" % h, align_bytes=64)
+                x_scales[z, part.start, part.stop] = tile[:]
             nc.vector.quantize_mx(
                 out=x_words[z][:, part].bitcast(FP8X4),
-                scales=x_scales[z, h][:],
+                scales=x_scales[z, part.start, part.stop],
                 in_=x_grouped[z, h][:].rearrange("p c t -> p (c t)"),
             )
 
+        w_grouped = {}
         w_words = {}
         w_scales = {}
-
-        def group_weights(b, m, passes, tag, on_vector=False):
-            name = "%d_%d_%d" % (b, m, passes[0])
-            width = len(passes) * P
-            grouped = keep.tile([P, width, PACK], BF16, name="w_grouped" + name, tag=tag, align_bytes=64)
-            words = keep.tile([P, width], U32, name="w_words" + name, align_bytes=64)
-            scales = keep.tile([P, width], U8, name="w_scales" + name, align_bytes=64)
-            for i, z in enumerate(passes):
-                cols = slice(i * P, (i + 1) * P)
-                dst = grouped[:, cols, :].rearrange("p (c i) t -> p c t i", i=4)
-                src = w_raw[b, m, z].rearrange("p t (c i) -> p c t i", i=4)
-                if on_vector:
-                    nc.vector.tensor_copy(out=dst, in_=src)
+        for m in (GATE, CAND):
+            for z in range(PASSES):
+                if (m, z) == (GATE, 0):
+                    for b in range(BLOCKS):
+                        tile = keep.tile([P, P, PACK], BF16, name="w_grouped0_0_%d" % b, align_bytes=64)
+                        w_grouped[m, z, b * P, (b + 1) * P] = tile[:]
                 else:
-                    nc.scalar.activation(out=dst, in_=src, func=ACT.Copy)
-                w_words[b, m, z] = words[:, cols]
-                w_scales[b, m, z] = scales[:, cols]
-            return grouped, words, scales
+                    tile = keep.tile([P, N, PACK], BF16, name="w_grouped%d_%d" % (m, z), align_bytes=64)
+                    w_grouped[m, z, 0, N] = tile[:]
+                    for b in range(BLOCKS):
+                        w_grouped[m, z, b * P, (b + 1) * P] = tile[:, b * P : (b + 1) * P, :]
+                w_words[m, z] = keep.tile([P, N], U32, name="w_words%d_%d" % (m, z), align_bytes=64)
+                w_scales[m, z] = keep.tile([P, N], U8, name="w_scales%d_%d" % (m, z), align_bytes=64)
+        both = slice(0, N)
+        block = [slice(b * P, (b + 1) * P) for b in range(BLOCKS)]
 
-        def quantise_weights(grouped, words, scales):
+        def round_weights(m, z, cols, on_vector):
+            dst = w_grouped[m, z, cols.start, cols.stop].rearrange("p (c i) t -> p c t i", i=4)
+            src = w_raw[m, z][:, :, cols].rearrange("p t (c i) -> p c t i", i=4)
+            if on_vector:
+                nc.vector.tensor_copy(out=dst, in_=src)
+            else:
+                nc.scalar.activation(out=dst, in_=src, func=ACT.Copy)
+
+        def quantise_weights(m, z, cols):
             nc.vector.quantize_mx(
-                out=words[:].bitcast(FP8X4), scales=scales[:], in_=grouped[:].rearrange("p c t -> p (c t)")
+                out=w_words[m, z][:, cols].bitcast(FP8X4),
+                scales=w_scales[m, z][:, cols],
+                in_=w_grouped[m, z, cols.start, cols.stop].rearrange("p c t -> p (c t)"),
             )
 
         acc = {}
 
-        def product(b, m, z, h, tag):
+        def product(b, m, z, part):
             if z == 0:
-                acc[b, m, h] = psum.tile([P, HALF], F32, name="acc%d_%d_%d" % (b, m, h), tag=tag)
+                acc[b, m, part.start] = psum.tile(
+                    [P, part.stop - part.start], F32, name="acc%d_%d_%d" % (b, m, part.start)
+                )
+            sums = acc[b, m, part.start][:] if b == 0 else acc[b, m, 0][:, part]
             nc.tensor.matmul_mx(
-                out=acc[b, m, h][:],
-                lhsT=w_words[b, m, z].bitcast(FP8X4),
-                lhsT_scale=w_scales[b, m, z],
-                rhs=x_words[z][:, halves[h]].bitcast(FP8X4),
-                rhs_scale=x_scales[z, h][:],
+                out=sums,
+                lhsT=w_words[m, z][:, block[b]].bitcast(FP8X4),
+                lhsT_scale=w_scales[m, z][:, block[b]],
+                rhs=x_words[z][:, part].bitcast(FP8X4),
+                rhs_scale=x_scales[z, part.start, part.stop],
                 start=(z == 0),
-                stop=(z == PASSES - 1),
+                stop=(z == PASSES - 1 and (b == 0 or part.stop == S)),
             )
 
-        whole = slice(0, S)
         for j in range(PACK - 1):
             gather_plane(0, j, whole)
         for h in halves:
             gather_plane(0, 3, h)
         for h in range(2):
-            weave(0, h, "x_grouped0_%d" % h)
+            weave(0, h)
         for h in range(2):
-            quantise_messages(0, h, "x_scales0_%d" % h)
+            quantise_messages(0, h)
         rounded = [keep.tile([P, T], BF16, name="rounded%d" % j) for j in range(2)]
-        for j in range(2):
-            nc.scalar.activation(out=rounded[j][:], in_=x_raw[1, j], func=ACT.Copy)
         by_scalar, by_vector = slice(0, 3 * QUARTER), slice(3 * QUARTER, S)
         for j in range(2):
+            nc.scalar.activation(out=rounded[j][:], in_=x_raw[1, j], func=ACT.Copy)
             nc.scalar.activation(
                 out=place(1, j, by_scalar), in_=rounded[j][:].indirect(entries(offs_sb, by_scalar)), func=ACT.Copy
             )
@@ -166,95 +171,83 @@ def tile_picked_gmem_relu_e_kernel(tc, xT, mem, w1, w2, offs, slot, out):
         gather_plane(1, 2, whole)
         for h in halves:
             gather_plane(1, 3, h)
-        weave(1, 0, "x_grouped1_0")
-        quantise_weights(*group_weights(0, GATE, [0], "gate_w0"))
-        quantise_messages(1, 0, "w_raw0_0_0")
-        quantise_weights(*group_weights(0, GATE, [1], "gate_w1"))
-        weave(1, 1, "w_raw0_0_1")
-        quantise_messages(1, 1, "x_scales1_1")
-        cand_w0 = [group_weights(0, CAND, [z], "cand_w%d" % z, on_vector=(z == PASSES - 1)) for z in range(PASSES)]
-        for tiles in cand_w0:
-            quantise_weights(*tiles)
         for h in range(2):
-            for z in range(PASSES):
-                product(0, GATE, z, h, "gate0_%d" % h)
-        for z in range(PASSES):
-            for h in range(2):
-                product(0, CAND, z, h, "cand0_%d" % h)
-
-        def sigmoids(b, parts, scale, name, given):
-            tiles = {}
-            for part in parts:
-                h, first = divmod(part.start, HALF)
-                width = part.stop - part.start
-                if part.start in given:
-                    dst = given[part.start]
-                else:
-                    tile = keep.tile([P, width], F32, name="%s%d_%d" % (name, b, part.start), align_bytes=64)
-                    dst = tile[:]
-                nc.scalar.activation(
-                    out=dst, in_=acc[b, GATE, h][:, first : first + width], func=ACT.Sigmoid, scale=scale
-                )
-                tiles[part.start] = dst
-            return tiles
-
-        def keep_old(dst, b, rest, part):
-            nc.vector.tensor_tensor(dst, mem_sb[b][:].indirect(entries(slot_sb, part)), rest[part.start], ALU.mult)
-
-        def make_fresh(dst, b, gate, part):
-            h, first = divmod(part.start, HALF)
-            cols = slice(first, first + part.stop - part.start)
-            nc.vector.scalar_tensor_tensor(
-                out=dst,
-                in0=acc[b, CAND, h][:, cols],
-                scalar=0.0,
-                in1=gate[h * HALF][:, cols],
-                op0=ALU.max,
-                op1=ALU.mult,
-            )
-
-        def put(b, kept, fresh, part):
-            nc.vector.tensor_tensor(mem_sb[b][:].indirect(entries(slot_sb, part)), kept, fresh, ALU.add)
-
-        third, fourth = slice(256, 320), slice(320, 512)
-        rest0 = sigmoids(0, [halves[0], third, fourth], -1.0, "rest", {0: fresh_ab[:, halves[0]]})
-        gate0 = sigmoids(0, halves, 1.0, "gate", {})
-
-        kept0 = keep.tile([P, S], F32, name="kept0")
-        for part in (halves[0], third, fourth):
-            keep_old(kept0[:, part], 0, rest0, part)
-        make_fresh(fresh_ab[:, PART_A], 0, gate0, PART_A)
-        make_fresh(fresh_ab[:, B_EARLY], 0, gate0, B_EARLY)
-        put(0, kept0[:, PART_A], fresh_ab[:, PART_A], PART_A)
-
-        gate_w = group_weights(1, GATE, [0, 1], "rest0_256")
-        cand_w = [group_weights(1, CAND, [z], "cand_w_b1_%d" % z) for z in range(PASSES)]
-        make_fresh(fresh_ab[:, B_LATE], 0, gate0, B_LATE)
-        quantise_weights(*gate_w)
-        for h in range(2):
-            for z in range(PASSES):
-                product(1, GATE, z, h, "gate1_%d" % h)
-        rest1 = sigmoids(1, halves, -1.0, "rest", {})
-        gate1 = sigmoids(1, halves, 1.0, "gate", {})
-        put(0, kept0[:, PART_B], fresh_ab[:, PART_B], PART_B)
-
-        fresh_c = keep.tile([P, PART_C.stop - PART_C.start], F32, name="fresh_c", tag="w_raw1_1_0", align_bytes=64)
-        make_fresh(fresh_c[:], 0, gate0, PART_C)
-        quantise_weights(*cand_w[0])
-        put(0, kept0[:, PART_C], fresh_c[:], PART_C)
-        quantise_weights(*cand_w[1])
-        for z in range(PASSES):
-            for h in range(2):
-                product(1, CAND, z, h, "cand1_%d" % h)
-        kept1 = keep.tile([P, S], F32, name="kept1")
-        fresh1 = keep.tile([P, S], F32, name="fresh1")
+            weave(1, h)
+        for b in range(BLOCKS):
+            round_weights(GATE, 0, block[b], False)
+        quantise_weights(GATE, 0, block[0])
+        quantise_messages(1, 0)
+        quantise_weights(GATE, 0, block[1])
+        quantise_messages(1, 1)
         for h in halves:
-            keep_old(kept1[:, h], 1, rest1, h)
-        make_fresh(fresh1[:, halves[0]], 1, gate1, halves[0])
-        fresh_d = keep.tile([P, PART_D.stop - PART_D.start], F32, name="fresh_d", tag="w_words1_1_1", align_bytes=64)
-        make_fresh(fresh_d[:], 0, gate0, PART_D)
-        make_fresh(fresh1[:, halves[1]], 1, gate1, halves[1])
-        put(0, kept0[:, PART_D], fresh_d[:], PART_D)
+            product(0, GATE, 0, h)
+        product(1, GATE, 0, whole)
+        round_weights(GATE, 1, block[0], False)
+        round_weights(GATE, 1, block[1], True)
+        for b in range(BLOCKS):
+            quantise_weights(GATE, 1, block[b])
+        for h in halves:
+            product(0, GATE, 1, h)
+        for h in halves:
+            product(1, GATE, 1, h)
+        round_weights(CAND, 0, block[0], False)
+        round_weights(CAND, 0, block[1], True)
+        quantise_weights(CAND, 0, both)
+        for h in halves:
+            product(0, CAND, 0, h)
+        product(1, CAND, 0, whole)
+
+        def sigmoid(b, scale, name, tag):
+            tile = keep.tile([P, S], F32, name=name, tag=tag, align_bytes=64)
+            for part in halves if b == 0 else [whole]:
+                nc.scalar.activation(out=tile[:, part], in_=acc[b, GATE, part.start][:], func=ACT.Sigmoid, scale=scale)
+            return tile
+
+        rest0 = sigmoid(0, -1.0, "rest0", "w_raw1_0")
+        gate0 = sigmoid(0, 1.0, "gate0", "w_grouped1_0")
+        for b in range(BLOCKS):
+            round_weights(CAND, 1, block[b], True)
+        for b in range(BLOCKS):
+            quantise_weights(CAND, 1, block[b])
+        for h in halves:
+            product(0, CAND, 1, h)
+        for h in halves:
+            product(1, CAND, 1, h)
+
+        old0 = keep.tile([P, HALF], F32, name="old0")
+        kept0 = keep.tile([P, S], F32, name="kept0")
+        fresh0 = keep.tile([P, S], F32, name="fresh0")
+        new0 = keep.tile([P, S], F32, name="new0")
+        old1 = keep.tile([P, S], F32, name="old1")
+        gap1 = keep.tile([P, S], F32, name="gap1")
+        step1 = keep.tile([P, S], F32, name="step1")
+
+        def look_up(dst, b, part):
+            nc.scalar.activation(out=dst, in_=mem_sb[b][:].indirect(entries(slot_sb, part)), func=ACT.Copy)
+
+        first, second = halves
+        nc.vector.tensor_tensor(
+            kept0[:, first], mem_sb[0][:].indirect(entries(slot_sb, first)), rest0[:, first], ALU.mult
+        )
+        look_up(old0[:], 0, second)
+        gate1 = sigmoid(1, 1.0, "gate1", "w_raw1_1")
+        for h in halves:
+            look_up(old1[:, h], 1, h)
+        for h in halves:
+            nc.vector.scalar_tensor_tensor(
+                out=fresh0[:, h], in0=acc[0, CAND, h.start][:], scalar=0.0, in1=gate0[:, h], op0=ALU.max, op1=ALU.mult
+            )
+        nc.vector.tensor_tensor(kept0[:, second], old0[:], rest0[:, second], ALU.mult)
+        for h in halves:
+            nc.vector.tensor_tensor(new0[:, h], kept0[:, h], fresh0[:, h], ALU.add)
+        for h in halves:
+            nc.scalar.activation(out=mem_sb[0][:].indirect(entries(slot_sb, h)), in_=new0[:, h], func=ACT.Copy)
         nc.sync.dma_start(out=out[0:P, :], in_=mem_sb[0][:])
-        put(1, kept1[:], fresh1[:], whole)
+        for h in halves:
+            nc.vector.scalar_tensor_tensor(
+                out=gap1[:, h], in0=acc[1, CAND, 0][:, h], scalar=0.0, in1=old1[:, h], op0=ALU.max, op1=ALU.subtract
+            )
+        for h in halves:
+            nc.vector.tensor_tensor(step1[:, h], gap1[:, h], gate1[:, h], ALU.mult)
+        nc.vector.tensor_tensor(mem_sb[1][:].indirect(slot_sb[:]), step1[:], old1[:], ALU.add)
         nc.sync.dma_start(out=out[P : 2 * P, :], in_=mem_sb[1][:])

@@ -39,6 +39,14 @@ def tile_picked_gmem_relu_e_kernel(tc, xT, mem, w1, w2, offs, slot, out):
         slot_sb = keep.tile([P, S // 16], U16, name="slot_sb")
 
         x_raw = {}
+        w_raw = {}
+
+        def load_weights(m, z):
+            raw = keep.tile([P, PACK * N], F32, name="w_raw%d_%d" % (m, z), align_bytes=64)
+            rows = (w2, w1)[m][z * K_PASS : (z + 1) * K_PASS, :]
+            nc.sync.dma_start(out=raw[:], in_=rows.rearrange("(p j) c -> p (j c)", j=PACK))
+            w_raw[m, z] = raw[:].rearrange("p (j c) -> p j c", j=PACK)
+
         for z in range(PASSES):
             rows = xT[z * K_PASS : (z + 1) * K_PASS, :].rearrange("(p j) t -> p j t", j=PACK)
             for j in range(PACK):
@@ -47,15 +55,11 @@ def tile_picked_gmem_relu_e_kernel(tc, xT, mem, w1, w2, offs, slot, out):
                 x_raw[z, j] = raw[:]
                 if (z, j) == (0, 0):
                     nc.sync.dma_start(offs_sb[:], offs)
-        w_raw = {}
-        for m in (GATE, CAND):
-            for z in range(PASSES):
-                raw = keep.tile([P, PACK * N], F32, name="w_raw%d_%d" % (m, z), align_bytes=64)
-                rows = (w2, w1)[m][z * K_PASS : (z + 1) * K_PASS, :]
-                nc.sync.dma_start(out=raw[:], in_=rows.rearrange("(p j) c -> p (j c)", j=PACK))
-                w_raw[m, z] = raw[:].rearrange("p (j c) -> p j c", j=PACK)
-            if m == GATE:
-                nc.sync.dma_start(slot_sb[:], slot)
+        for z in range(PASSES):
+            load_weights(GATE, z)
+        nc.sync.dma_start(slot_sb[:], slot)
+        for z in range(PASSES):
+            load_weights(CAND, z)
         mem_sb = []
         for b in range(BLOCKS):
             mem_b = keep.tile([P, U], F32, name="mem%d" % b)
@@ -67,7 +71,7 @@ def tile_picked_gmem_relu_e_kernel(tc, xT, mem, w1, w2, offs, slot, out):
 
         whole = slice(0, S)
         halves = [slice(0, HALF), slice(HALF, S)]
-        pairs = [keep.tile([P, 4, 2, QUARTER, 2], BF16, name="pairs%d" % z) for z in range(PASSES)]
+        pairs = [keep.tile([P, 2 + z, 2, QUARTER, 2], BF16, name="pairs%d" % z) for z in range(PASSES)]
         x_grouped = {}
         x_words = [keep.tile([P, S], U32, name="x_words%d" % z, align_bytes=64) for z in range(PASSES)]
         scales0 = keep.tile([P, S], U8, name="x_scales0", align_bytes=64)
@@ -79,20 +83,20 @@ def tile_picked_gmem_relu_e_kernel(tc, xT, mem, w1, w2, offs, slot, out):
         def gather_plane(z, j, part):
             nc.vector.tensor_copy(out=place(z, j, part), in_=x_raw[z, j].indirect(entries(offs_sb, part)))
 
-        def weave(z, h):
-            x_grouped[z, h] = keep.tile([P, HALF, PACK], BF16, name="x_grouped%d_%d" % (z, h), align_bytes=64)
+        def weave(z, dst, quarters):
+            count = quarters.stop - quarters.start
             nc.vector.tensor_copy(
-                out=x_grouped[z, h][:].rearrange("p c t -> p (c t)").bitcast(I32).rearrange("p (q c u) -> p q c u", q=2, u=2),
-                in_=pairs[z][:, 2 * h : 2 * h + 2]
+                out=dst.rearrange("p c t -> p (c t)").bitcast(I32).rearrange("p (q c u) -> p q c u", q=count, u=2),
+                in_=pairs[z][:, quarters]
                 .rearrange("p q u c e -> p (q u c e)")
                 .bitcast(I32)
-                .rearrange("p (q u c) -> p q c u", q=2, u=2),
+                .rearrange("p (q u c) -> p q c u", q=count, u=2),
             )
 
         def quantise_messages(z, h):
             part = halves[h]
             if z == 1:
-                tile = keep.tile([P, HALF], U8, name="x_scales1_%d" % h, tag="w_grouped0_0_%d" % h, align_bytes=64)
+                tile = keep.tile([P, HALF], U8, name="x_scales1_%d" % h, tag=("x_scales1_0", "w_grouped0_0_0")[h], align_bytes=64)
                 x_scales[z, part.start, part.stop] = tile[:]
             nc.vector.quantize_mx(
                 out=x_words[z][:, part].bitcast(FP8X4),
@@ -103,99 +107,108 @@ def tile_picked_gmem_relu_e_kernel(tc, xT, mem, w1, w2, offs, slot, out):
         w_grouped = {}
         w_words = {}
         w_scales = {}
+
+        def weight_tiles(members):
+            name = "%d_%d_%d" % members[0]
+            width = len(members) * P
+            grouped = keep.tile([P, width, PACK], BF16, name="w_grouped" + name, align_bytes=64)
+            words = keep.tile([P, width], U32, name="w_words" + name, align_bytes=64)
+            scales = keep.tile([P, width], U8, name="w_scales" + name, align_bytes=64)
+            for i, member in enumerate(members):
+                cols = slice(i * P, (i + 1) * P)
+                w_grouped[member] = grouped[:, cols, :]
+                w_words[member] = words[:, cols]
+                w_scales[member] = scales[:, cols]
+            return grouped, words, scales
+
+        last_cand = [(CAND, 0, 1), (CAND, 1, 1)]
+        w_tiles = {last_cand[0]: weight_tiles(last_cand)}
         for m in (GATE, CAND):
             for z in range(PASSES):
-                if (m, z) == (GATE, 0):
-                    for b in range(BLOCKS):
-                        tile = keep.tile([P, P, PACK], BF16, name="w_grouped0_0_%d" % b, align_bytes=64)
-                        w_grouped[m, z, b * P, (b + 1) * P] = tile[:]
-                else:
-                    tile = keep.tile([P, N, PACK], BF16, name="w_grouped%d_%d" % (m, z), align_bytes=64)
-                    w_grouped[m, z, 0, N] = tile[:]
-                    for b in range(BLOCKS):
-                        w_grouped[m, z, b * P, (b + 1) * P] = tile[:, b * P : (b + 1) * P, :]
-                w_words[m, z] = keep.tile([P, N], U32, name="w_words%d_%d" % (m, z), align_bytes=64)
-                w_scales[m, z] = keep.tile([P, N], U8, name="w_scales%d_%d" % (m, z), align_bytes=64)
-        both = slice(0, N)
-        block = [slice(b * P, (b + 1) * P) for b in range(BLOCKS)]
+                for b in range(BLOCKS):
+                    if (m, z, b) not in last_cand:
+                        w_tiles[m, z, b] = weight_tiles([(m, z, b)])
 
-        def round_weights(m, z, cols, on_vector):
-            dst = w_grouped[m, z, cols.start, cols.stop].rearrange("p (c i) t -> p c t i", i=4)
-            src = w_raw[m, z][:, :, cols].rearrange("p t (c i) -> p c t i", i=4)
+        def round_weights(m, z, b, on_vector):
+            dst = w_grouped[m, z, b].rearrange("p (c i) t -> p c t i", i=4)
+            src = w_raw[m, z][:, :, b * P : (b + 1) * P].rearrange("p t (c i) -> p c t i", i=4)
             if on_vector:
                 nc.vector.tensor_copy(out=dst, in_=src)
             else:
                 nc.scalar.activation(out=dst, in_=src, func=ACT.Copy)
 
-        def quantise_weights(m, z, cols):
+        def quantise_weights(m, z, b):
+            grouped, words, scales = w_tiles[m, z, b]
             nc.vector.quantize_mx(
-                out=w_words[m, z][:, cols].bitcast(FP8X4),
-                scales=w_scales[m, z][:, cols],
-                in_=w_grouped[m, z, cols.start, cols.stop].rearrange("p c t -> p (c t)"),
+                out=words[:].bitcast(FP8X4), scales=scales[:], in_=grouped[:].rearrange("p c t -> p (c t)")
             )
 
         acc = {}
 
         def product(b, m, z, part):
-            if z == 0:
+            opens = z == 0 and (b == 0 or part.start == 0)
+            if opens:
                 acc[b, m, part.start] = psum.tile(
-                    [P, part.stop - part.start], F32, name="acc%d_%d_%d" % (b, m, part.start)
+                    [P, HALF if b == 0 else S], F32, name="acc%d_%d_%d" % (b, m, part.start)
                 )
             sums = acc[b, m, part.start][:] if b == 0 else acc[b, m, 0][:, part]
             nc.tensor.matmul_mx(
                 out=sums,
-                lhsT=w_words[m, z][:, block[b]].bitcast(FP8X4),
-                lhsT_scale=w_scales[m, z][:, block[b]],
+                lhsT=w_words[m, z, b].bitcast(FP8X4),
+                lhsT_scale=w_scales[m, z, b],
                 rhs=x_words[z][:, part].bitcast(FP8X4),
                 rhs_scale=x_scales[z, part.start, part.stop],
-                start=(z == 0),
+                start=opens,
                 stop=(z == PASSES - 1 and (b == 0 or part.stop == S)),
             )
 
-        for j in range(PACK - 1):
-            gather_plane(0, j, whole)
-        for h in halves:
-            gather_plane(0, 3, h)
-        for h in range(2):
-            weave(0, h)
-        for h in range(2):
-            quantise_messages(0, h)
-        rounded = [keep.tile([P, T], BF16, name="rounded%d" % j) for j in range(2)]
-        by_scalar, by_vector = slice(0, 3 * QUARTER), slice(3 * QUARTER, S)
-        for j in range(2):
-            nc.scalar.activation(out=rounded[j][:], in_=x_raw[1, j], func=ACT.Copy)
-            nc.scalar.activation(
-                out=place(1, j, by_scalar), in_=rounded[j][:].indirect(entries(offs_sb, by_scalar)), func=ACT.Copy
+        for z in range(PASSES):
+            quarters = (2, 3)[z]
+            by_vector, by_scalar = slice(0, quarters * QUARTER), slice(quarters * QUARTER, S)
+            planes = keep.tile([P, PACK, S - by_scalar.start], BF16, name="planes%d" % z, align_bytes=64)
+            for j in range(PACK):
+                nc.scalar.activation(
+                    out=planes[:, j, :], in_=x_raw[z, j].indirect(entries(offs_sb, by_scalar)), func=ACT.Copy
+                )
+                if j < PACK - 1 or quarters == 2:
+                    gather_plane(z, j, by_vector)
+                else:
+                    gather_plane(z, j, halves[0])
+                    gather_plane(z, j, slice(HALF, by_vector.stop))
+            for h in range(2):
+                x_grouped[z, h] = keep.tile([P, HALF, PACK], BF16, name="x_grouped%d_%d" % (z, h), align_bytes=64)
+            weave(z, x_grouped[z, 0][:], slice(0, 2))
+            if quarters == 3:
+                weave(z, x_grouped[z, 1][:, :QUARTER, :], slice(2, 3))
+            nc.scalar.copy(
+                out=x_grouped[z, 1][:, by_scalar.start - HALF :, :].rearrange("p (c i) t -> p c t i", i=4),
+                in_=planes[:].rearrange("p t (c i) -> p c t i", i=4),
             )
-            gather_plane(1, j, by_vector)
-        gather_plane(1, 2, whole)
-        for h in halves:
-            gather_plane(1, 3, h)
-        for h in range(2):
-            weave(1, h)
+            if z == 0:
+                for h in range(2):
+                    quantise_messages(0, h)
         for b in range(BLOCKS):
-            round_weights(GATE, 0, block[b], False)
-        quantise_weights(GATE, 0, block[0])
+            round_weights(GATE, 0, b, False)
         quantise_messages(1, 0)
-        quantise_weights(GATE, 0, block[1])
+        quantise_weights(GATE, 0, 0)
         quantise_messages(1, 1)
+        round_weights(GATE, 1, 0, True)
+        round_weights(GATE, 1, 1, False)
+        quantise_weights(GATE, 0, 1)
+        quantise_weights(GATE, 1, 0)
         for h in halves:
             product(0, GATE, 0, h)
         product(1, GATE, 0, whole)
-        round_weights(GATE, 1, block[0], False)
-        round_weights(GATE, 1, block[1], True)
-        for b in range(BLOCKS):
-            quantise_weights(GATE, 1, block[b])
         for h in halves:
             product(0, GATE, 1, h)
+        round_weights(CAND, 0, 0, True)
+        round_weights(CAND, 0, 1, False)
+        quantise_weights(GATE, 1, 1)
+        quantise_weights(CAND, 0, 0)
         for h in halves:
             product(1, GATE, 1, h)
-        round_weights(CAND, 0, block[0], False)
-        round_weights(CAND, 0, block[1], True)
-        quantise_weights(CAND, 0, both)
         for h in halves:
             product(0, CAND, 0, h)
-        product(1, CAND, 0, whole)
 
         def sigmoid(b, scale, name, tag):
             tile = keep.tile([P, S], F32, name=name, tag=tag, align_bytes=64)
@@ -204,13 +217,14 @@ def tile_picked_gmem_relu_e_kernel(tc, xT, mem, w1, w2, offs, slot, out):
             return tile
 
         rest0 = sigmoid(0, -1.0, "rest0", "w_raw1_0")
-        gate0 = sigmoid(0, 1.0, "gate0", "w_grouped1_0")
+        gate0 = sigmoid(0, 1.0, "gate0", "w_grouped1_0_0")
         for b in range(BLOCKS):
-            round_weights(CAND, 1, block[b], True)
-        for b in range(BLOCKS):
-            quantise_weights(CAND, 1, block[b])
+            round_weights(CAND, 1, b, True)
+        quantise_weights(CAND, 1, 0)
+        quantise_weights(CAND, 0, 1)
         for h in halves:
             product(0, CAND, 1, h)
+        product(1, CAND, 0, whole)
         for h in halves:
             product(1, CAND, 1, h)
 

@@ -42,7 +42,7 @@ def tile_picked_gmem_relu_e_kernel(tc, xT, mem, w1, w2, offs, slot, out):
         w_raw = {}
 
         def load_weights(m, z):
-            raw = keep.tile([P, PACK * N], F32, name="w_raw%d_%d" % (m, z), align_bytes=64)
+            raw = keep.tile([P, PACK * N], F32, name="w_raw%d_%d" % (m, z), align_bytes=256)
             rows = (w2, w1)[m][z * K_PASS : (z + 1) * K_PASS, :]
             nc.sync.dma_start(out=raw[:], in_=rows.rearrange("(p j) c -> p (j c)", j=PACK))
             w_raw[m, z] = raw[:].rearrange("p (j c) -> p j c", j=PACK)
@@ -50,7 +50,7 @@ def tile_picked_gmem_relu_e_kernel(tc, xT, mem, w1, w2, offs, slot, out):
         for z in range(PASSES):
             rows = xT[z * K_PASS : (z + 1) * K_PASS, :].rearrange("(p j) t -> p j t", j=PACK)
             for j in range(PACK):
-                raw = keep.tile([P, T], F32, name="x_raw%d_%d" % (z, j), align_bytes=64)
+                raw = keep.tile([P, T], F32, name="x_raw%d_%d" % (z, j), align_bytes=256)
                 nc.sync.dma_start(out=raw[:], in_=rows[:, j, :])
                 x_raw[z, j] = raw[:]
                 if (z, j) == (0, 0):
@@ -62,7 +62,7 @@ def tile_picked_gmem_relu_e_kernel(tc, xT, mem, w1, w2, offs, slot, out):
             load_weights(CAND, z)
         mem_sb = []
         for b in range(BLOCKS):
-            mem_b = keep.tile([P, U], F32, name="mem%d" % b)
+            mem_b = keep.tile([P, U], F32, name="mem%d" % b, align_bytes=256)
             nc.sync.dma_start(out=mem_b[:], in_=mem[b * P : (b + 1) * P, :])
             mem_sb.append(mem_b)
 
@@ -210,14 +210,14 @@ def tile_picked_gmem_relu_e_kernel(tc, xT, mem, w1, w2, offs, slot, out):
         for h in halves:
             product(0, CAND, 0, h)
 
-        def sigmoid(b, scale, name, tag):
-            tile = keep.tile([P, S], F32, name=name, tag=tag, align_bytes=64)
+        def sigmoid(b, scale, name, tag, align):
+            tile = keep.tile([P, S], F32, name=name, tag=tag, align_bytes=align)
             for part in halves if b == 0 else [whole]:
                 nc.scalar.activation(out=tile[:, part], in_=acc[b, GATE, part.start][:], func=ACT.Sigmoid, scale=scale)
             return tile
 
-        rest0 = sigmoid(0, -1.0, "rest0", "w_raw1_0")
-        gate0 = sigmoid(0, 1.0, "gate0", "w_grouped1_0_0")
+        rest0 = sigmoid(0, -1.0, "rest0", "w_raw1_0", 256)
+        gate0 = sigmoid(0, 1.0, "gate0", "w_grouped1_0_0", 64)
         for b in range(BLOCKS):
             round_weights(CAND, 1, b, True)
         quantise_weights(CAND, 1, 0)
@@ -244,7 +244,7 @@ def tile_picked_gmem_relu_e_kernel(tc, xT, mem, w1, w2, offs, slot, out):
             kept0[:, first], mem_sb[0][:].indirect(entries(slot_sb, first)), rest0[:, first], ALU.mult
         )
         look_up(old0[:], 0, second)
-        gate1 = sigmoid(1, 1.0, "gate1", "w_raw1_1")
+        gate1 = sigmoid(1, 1.0, "gate1", "w_raw1_1", 256)
         for h in halves:
             look_up(old1[:, h], 1, h)
         for h in halves:

@@ -231,7 +231,7 @@ def tile_picked_gmem_relu_e_kernel(tc, xT, mem, w1, w2, offs, slot, out):
         old0 = keep.tile([P, HALF], F32, name="old0")
         kept0 = keep.tile([P, S], F32, name="kept0")
         fresh0 = keep.tile([P, S], F32, name="fresh0")
-        new0 = keep.tile([P, S], F32, name="new0")
+        new0 = keep.tile([P, HALF], F32, name="new0")
         old1 = keep.tile([P, S], F32, name="old1")
         gap1 = keep.tile([P, S], F32, name="gap1")
         step1 = keep.tile([P, S], F32, name="step1")
@@ -252,16 +252,16 @@ def tile_picked_gmem_relu_e_kernel(tc, xT, mem, w1, w2, offs, slot, out):
                 out=fresh0[:, h], in0=acc[0, CAND, h.start][:], scalar=0.0, in1=gate0[:, h], op0=ALU.max, op1=ALU.mult
             )
         nc.vector.tensor_tensor(kept0[:, second], old0[:], rest0[:, second], ALU.mult)
-        for h in halves:
-            nc.vector.tensor_tensor(new0[:, h], kept0[:, h], fresh0[:, h], ALU.add)
-        for h in halves:
-            nc.scalar.activation(out=mem_sb[0][:].indirect(entries(slot_sb, h)), in_=new0[:, h], func=ACT.Copy)
-        nc.sync.dma_start(out=out[0:P, :], in_=mem_sb[0][:])
+        nc.vector.tensor_tensor(new0[:], kept0[:, first], fresh0[:, first], ALU.add)
+        nc.scalar.activation(out=mem_sb[0][:].indirect(entries(slot_sb, first)), in_=new0[:], func=ACT.Copy)
         for h in halves:
             nc.vector.scalar_tensor_tensor(
                 out=gap1[:, h], in0=acc[1, CAND, 0][:, h], scalar=0.0, in1=old1[:, h], op0=ALU.max, op1=ALU.subtract
             )
         for h in halves:
             nc.vector.tensor_tensor(step1[:, h], gap1[:, h], gate1[:, h], ALU.mult)
+        nc.vector.tensor_tensor(gap1[:, first], kept0[:, second], fresh0[:, second], ALU.add)
+        nc.scalar.activation(out=mem_sb[0][:].indirect(entries(slot_sb, second)), in_=gap1[:, first], func=ACT.Copy)
+        nc.sync.dma_start(out=out[0:P, :], in_=mem_sb[0][:])
         nc.vector.tensor_tensor(mem_sb[1][:].indirect(slot_sb[:]), step1[:], old1[:], ALU.add)
         nc.sync.dma_start(out=out[P : 2 * P, :], in_=mem_sb[1][:])

@@ -210,18 +210,19 @@ def tile_picked_gmem_relu_e_kernel(tc, xT, mem, w1, w2, offs, slot, out):
         for h in halves:
             product(0, CAND, 0, h)
 
-        def sigmoid(b, scale, name, tag, align):
-            tile = keep.tile([P, S], F32, name=name, tag=tag, align_bytes=align)
+        def sigmoid(b, name, tag):
+            tile = keep.tile([P, S], F32, name=name, tag=tag, align_bytes=256)
             for part in halves if b == 0 else [whole]:
-                nc.scalar.activation(out=tile[:, part], in_=acc[b, GATE, part.start][:], func=ACT.Sigmoid, scale=scale)
+                nc.scalar.activation(out=tile[:, part], in_=acc[b, GATE, part.start][:], func=ACT.Sigmoid)
             return tile
 
-        rest0 = sigmoid(0, -1.0, "rest0", "w_raw1_0", 256)
-        gate0 = sigmoid(0, 1.0, "gate0", "w_grouped1_0_0", 64)
+        gate0 = sigmoid(0, "gate0", "w_raw1_0")
         for b in range(BLOCKS):
             round_weights(CAND, 1, b, True)
         quantise_weights(CAND, 1, 0)
         quantise_weights(CAND, 0, 1)
+        rest0 = keep.tile([P, S], F32, name="rest0", tag="w_grouped1_1_0", align_bytes=64)
+        nc.vector.tensor_scalar(out=rest0[:], in0=gate0[:], scalar1=-1.0, scalar2=1.0, op0=ALU.mult, op1=ALU.add)
         for h in halves:
             product(0, CAND, 1, h)
         product(1, CAND, 0, whole)
@@ -244,15 +245,15 @@ def tile_picked_gmem_relu_e_kernel(tc, xT, mem, w1, w2, offs, slot, out):
             kept0[:, first], mem_sb[0][:].indirect(entries(slot_sb, first)), rest0[:, first], ALU.mult
         )
         look_up(old0[:], 0, second)
-        gate1 = sigmoid(1, 1.0, "gate1", "w_raw1_1", 256)
+        gate1 = sigmoid(1, "gate1", "w_raw1_1")
         for h in halves:
             look_up(old1[:, h], 1, h)
         for h in halves:
             nc.vector.scalar_tensor_tensor(
                 out=fresh0[:, h], in0=acc[0, CAND, h.start][:], scalar=0.0, in1=gate0[:, h], op0=ALU.max, op1=ALU.mult
             )
-        nc.vector.tensor_tensor(kept0[:, second], old0[:], rest0[:, second], ALU.mult)
         nc.vector.tensor_tensor(new0[:], kept0[:, first], fresh0[:, first], ALU.add)
+        nc.vector.tensor_tensor(kept0[:, second], old0[:], rest0[:, second], ALU.mult)
         nc.scalar.activation(out=mem_sb[0][:].indirect(entries(slot_sb, first)), in_=new0[:], func=ACT.Copy)
         for h in halves:
             nc.vector.scalar_tensor_tensor(

@@ -22,7 +22,8 @@ PASSES = K // K_PASS
 BLOCKS = N // P
 GATE, CAND = 0, 1
 HALF = S // 2
-QUARTER = S // 4
+LEAD = 192
+PIECE = LEAD // 2
 
 
 def entries(list_sb, part):
@@ -39,103 +40,99 @@ def tile_picked_gmem_relu_e_kernel(tc, xT, mem, w1, w2, offs, slot, out):
         slot_sb = keep.tile([P, S // 16], U16, name="slot_sb")
 
         x_raw = {}
+        rows = xT[:K_PASS, :].rearrange("(p u a) t -> p u (a t)", u=2, a=2)
+        for u in range(2):
+            x_raw[0, u] = keep.tile([P, 2 * T], F32, name="x_raw0_%d" % u, align_bytes=256)
+            nc.sync.dma_start(out=x_raw[0, u][:], in_=rows[:, u, :])
+            if u == 0:
+                nc.sync.dma_start(offs_sb[:], offs)
+        rows = xT[K_PASS:, :].rearrange("(p j) t -> p j t", j=PACK)
+        for j in range(PACK):
+            x_raw[1, j] = keep.tile([P, T], F32, name="x_raw1_%d" % j, align_bytes=256)
+            nc.sync.dma_start(out=x_raw[1, j][:], in_=rows[:, j, :])
         w_raw = {}
-
-        def load_weights(m, z):
-            raw = keep.tile([P, PACK * N], F32, name="w_raw%d_%d" % (m, z), align_bytes=256)
-            rows = (w2, w1)[m][z * K_PASS : (z + 1) * K_PASS, :]
-            nc.sync.dma_start(out=raw[:], in_=rows.rearrange("(p j) c -> p (j c)", j=PACK))
-            w_raw[m, z] = raw[:].rearrange("p (j c) -> p j c", j=PACK)
-
-        for z in range(PASSES):
-            rows = xT[z * K_PASS : (z + 1) * K_PASS, :].rearrange("(p j) t -> p j t", j=PACK)
-            for j in range(PACK):
-                raw = keep.tile([P, T], F32, name="x_raw%d_%d" % (z, j), align_bytes=256)
-                nc.sync.dma_start(out=raw[:], in_=rows[:, j, :])
-                x_raw[z, j] = raw[:]
-                if (z, j) == (0, 0):
-                    nc.sync.dma_start(offs_sb[:], offs)
-        for z in range(PASSES):
-            load_weights(GATE, z)
-        nc.sync.dma_start(slot_sb[:], slot)
-        for z in range(PASSES):
-            load_weights(CAND, z)
+        for m in (GATE, CAND):
+            for z in range(PASSES):
+                raw = keep.tile([P, PACK * N], F32, name="w_raw%d_%d" % (m, z), align_bytes=256)
+                rows = (w2, w1)[m][z * K_PASS : (z + 1) * K_PASS, :]
+                nc.sync.dma_start(out=raw[:], in_=rows.rearrange("(p j) c -> p (j c)", j=PACK))
+                w_raw[m, z] = raw[:].rearrange("p (u a c) -> p u a c", u=2, a=2)
+            if m == GATE:
+                nc.sync.dma_start(slot_sb[:], slot)
         mem_sb = []
         for b in range(BLOCKS):
             mem_b = keep.tile([P, U], F32, name="mem%d" % b, align_bytes=256)
             nc.sync.dma_start(out=mem_b[:], in_=mem[b * P : (b + 1) * P, :])
             mem_sb.append(mem_b)
 
+        zero = keep.tile([P, 1], F32, name="zero")
         warm = keep.tile([P, 1], F32, name="warm")
-        nc.scalar.activation(out=warm[:], in_=x_raw[0, 0][:, 0:1], func=ACT.Sigmoid)
+        nc.vector.memset(zero[:], 0.0)
+        nc.scalar.activation(out=warm[:], in_=zero[:], func=ACT.Sigmoid)
 
         whole = slice(0, S)
         halves = [slice(0, HALF), slice(HALF, S)]
-        pairs = [keep.tile([P, 2 + z, 2, QUARTER, 2], BF16, name="pairs%d" % z) for z in range(PASSES)]
-        x_grouped = {}
+        first, second = halves
         x_words = [keep.tile([P, S], U32, name="x_words%d" % z, align_bytes=64) for z in range(PASSES)]
-        scales0 = keep.tile([P, S], U8, name="x_scales0", align_bytes=64)
-        x_scales = {(0, 0, HALF): scales0[:, :HALF], (0, HALF, S): scales0[:, HALF:], (0, 0, S): scales0[:]}
+        x_scales = [keep.tile([P, S], U8, name="x_scales%d" % z, align_bytes=64) for z in range(PASSES)]
+        x_grouped = [keep.tile([P, S * PACK], BF16, name="x_grouped%d" % z, align_bytes=64) for z in range(PASSES)]
 
-        def place(z, j, part):
-            return pairs[z][:, part.start // QUARTER : part.stop // QUARTER, j // 2, :, j % 2]
-
-        def gather_plane(z, j, part):
-            nc.vector.tensor_copy(out=place(z, j, part), in_=x_raw[z, j].indirect(entries(offs_sb, part)))
-
-        def weave(z, dst, quarters):
-            count = quarters.stop - quarters.start
-            nc.vector.tensor_copy(
-                out=dst.rearrange("p c t -> p (c t)").bitcast(I32).rearrange("p (q c u) -> p q c u", q=count, u=2),
-                in_=pairs[z][:, quarters]
-                .rearrange("p q u c e -> p (q u c e)")
-                .bitcast(I32)
-                .rearrange("p (q u c) -> p q c u", q=count, u=2),
-            )
-
-        def quantise_messages(z, h):
-            part = halves[h]
-            if z == 1:
-                tile = keep.tile([P, HALF], U8, name="x_scales1_%d" % h, tag=("x_scales1_0", "w_grouped0_0_0")[h], align_bytes=64)
-                x_scales[z, part.start, part.stop] = tile[:]
+        def quantise_messages(z, part):
             nc.vector.quantize_mx(
                 out=x_words[z][:, part].bitcast(FP8X4),
-                scales=x_scales[z, part.start, part.stop],
-                in_=x_grouped[z, h][:].rearrange("p c t -> p (c t)"),
+                scales=x_scales[z][:, part],
+                in_=x_grouped[z][:, part.start * PACK : part.stop * PACK],
             )
+
+        for z in range(PASSES):
+            pairs = [keep.tile([P, 2, HALF, 2], BF16, name="pairs%d_%d" % (z, h)) for h in range(2)]
+            for u in range(2):
+                for i in range(2):
+                    if z == 0:
+                        picked = entries(offs_sb, halves[i])
+                        by_scalar = pairs[i][:, 0, :, u], x_raw[0, u][:].indirect(picked)
+                        by_vector = pairs[i][:, 1, :, u], x_raw[0, u][:, T:].indirect(picked)
+                    else:
+                        plane = x_raw[1, 2 * u + i]
+                        by_scalar = pairs[1][:, i, :, u], plane[:].indirect(entries(offs_sb, second))
+                        by_vector = pairs[0][:, i, :, u], plane[:].indirect(entries(offs_sb, first))
+                    nc.scalar.activation(out=by_scalar[0], in_=by_scalar[1], func=ACT.Copy)
+                    nc.vector.tensor_copy(out=by_vector[0], in_=by_vector[1])
+            for h in range(2):
+                nc.vector.tensor_copy(
+                    out=x_grouped[z][:, h * HALF * PACK : (h + 1) * HALF * PACK]
+                    .bitcast(I32)
+                    .rearrange("p (c a) -> p c a", a=2),
+                    in_=pairs[h][:].rearrange("p a c u -> p (a c u)").bitcast(I32).rearrange("p (a c) -> p c a", a=2),
+                )
+            if z == 0:
+                quantise_messages(0, whole)
 
         w_grouped = {}
         w_words = {}
         w_scales = {}
-
-        def weight_tiles(members):
-            name = "%d_%d_%d" % members[0]
+        w_tiles = {}
+        groups = [[(m, z, b)] for m in (GATE, CAND) for z in range(PASSES) for b in range(BLOCKS)]
+        for members in groups:
+            name = "%d_%d_%d" % members[-1]
             width = len(members) * P
             grouped = keep.tile([P, width, PACK], BF16, name="w_grouped" + name, align_bytes=64)
             words = keep.tile([P, width], U32, name="w_words" + name, align_bytes=64)
             scales = keep.tile([P, width], U8, name="w_scales" + name, align_bytes=64)
+            w_tiles[members[-1]] = grouped, words, scales
             for i, member in enumerate(members):
                 cols = slice(i * P, (i + 1) * P)
                 w_grouped[member] = grouped[:, cols, :]
                 w_words[member] = words[:, cols]
                 w_scales[member] = scales[:, cols]
-            return grouped, words, scales
-
-        last_cand = [(CAND, 0, 1), (CAND, 1, 1)]
-        w_tiles = {last_cand[0]: weight_tiles(last_cand)}
-        for m in (GATE, CAND):
-            for z in range(PASSES):
-                for b in range(BLOCKS):
-                    if (m, z, b) not in last_cand:
-                        w_tiles[m, z, b] = weight_tiles([(m, z, b)])
 
         def round_weights(m, z, b, on_vector):
-            dst = w_grouped[m, z, b].rearrange("p (c i) t -> p c t i", i=4)
-            src = w_raw[m, z][:, :, b * P : (b + 1) * P].rearrange("p t (c i) -> p c t i", i=4)
+            dst = w_grouped[m, z, b].rearrange("p (c i) (a u) -> p c a u i", i=4, u=2)
+            src = w_raw[m, z][:, :, :, b * P : (b + 1) * P].rearrange("p u a (c i) -> p c a u i", i=4)
             if on_vector:
                 nc.vector.tensor_copy(out=dst, in_=src)
             else:
-                nc.scalar.activation(out=dst, in_=src, func=ACT.Copy)
+                nc.scalar.copy(out=dst, in_=src)
 
         def quantise_weights(m, z, b):
             grouped, words, scales = w_tiles[m, z, b]
@@ -146,123 +143,115 @@ def tile_picked_gmem_relu_e_kernel(tc, xT, mem, w1, w2, offs, slot, out):
         acc = {}
 
         def product(b, m, z, part):
-            opens = z == 0 and (b == 0 or part.start == 0)
+            opens = z == (1 if (b, m) == (1, CAND) else 0)
             if opens:
                 acc[b, m, part.start] = psum.tile(
-                    [P, HALF if b == 0 else S], F32, name="acc%d_%d_%d" % (b, m, part.start)
+                    [P, part.stop - part.start], F32, name="acc%d_%d_%d" % (b, m, part.start)
                 )
-            sums = acc[b, m, part.start][:] if b == 0 else acc[b, m, 0][:, part]
             nc.tensor.matmul_mx(
-                out=sums,
+                out=acc[b, m, part.start][:],
                 lhsT=w_words[m, z, b].bitcast(FP8X4),
                 lhsT_scale=w_scales[m, z, b],
                 rhs=x_words[z][:, part].bitcast(FP8X4),
-                rhs_scale=x_scales[z, part.start, part.stop],
+                rhs_scale=x_scales[z][:, part],
                 start=opens,
-                stop=(z == PASSES - 1 and (b == 0 or part.stop == S)),
+                stop=not opens,
             )
 
-        for z in range(PASSES):
-            quarters = (2, 3)[z]
-            by_vector, by_scalar = slice(0, quarters * QUARTER), slice(quarters * QUARTER, S)
-            planes = keep.tile([P, PACK, S - by_scalar.start], BF16, name="planes%d" % z, align_bytes=64)
-            for j in range(PACK):
-                nc.scalar.activation(
-                    out=planes[:, j, :], in_=x_raw[z, j].indirect(entries(offs_sb, by_scalar)), func=ACT.Copy
-                )
-                if j < PACK - 1 or quarters == 2:
-                    gather_plane(z, j, by_vector)
-                else:
-                    gather_plane(z, j, halves[0])
-                    gather_plane(z, j, slice(HALF, by_vector.stop))
-            for h in range(2):
-                x_grouped[z, h] = keep.tile([P, HALF, PACK], BF16, name="x_grouped%d_%d" % (z, h), align_bytes=64)
-            weave(z, x_grouped[z, 0][:], slice(0, 2))
-            if quarters == 3:
-                weave(z, x_grouped[z, 1][:, :QUARTER, :], slice(2, 3))
-            nc.scalar.copy(
-                out=x_grouped[z, 1][:, by_scalar.start - HALF :, :].rearrange("p (c i) t -> p c t i", i=4),
-                in_=planes[:].rearrange("p t (c i) -> p c t i", i=4),
-            )
-            if z == 0:
-                for h in range(2):
-                    quantise_messages(0, h)
+        def products(b, m, z):
+            for part in halves if b == 0 else [whole]:
+                product(b, m, z, part)
+
         for b in range(BLOCKS):
             round_weights(GATE, 0, b, False)
-        quantise_messages(1, 0)
+        for h in halves:
+            quantise_messages(1, h)
         quantise_weights(GATE, 0, 0)
-        quantise_messages(1, 1)
         round_weights(GATE, 1, 0, True)
         round_weights(GATE, 1, 1, False)
         quantise_weights(GATE, 0, 1)
-        quantise_weights(GATE, 1, 0)
-        for h in halves:
-            product(0, GATE, 0, h)
-        product(1, GATE, 0, whole)
-        for h in halves:
-            product(0, GATE, 1, h)
+        for b in range(BLOCKS):
+            quantise_weights(GATE, 1, b)
+        for z in range(PASSES):
+            for b in range(BLOCKS):
+                products(b, GATE, z)
         round_weights(CAND, 0, 0, True)
         round_weights(CAND, 0, 1, False)
-        quantise_weights(GATE, 1, 1)
-        quantise_weights(CAND, 0, 0)
-        for h in halves:
-            product(1, GATE, 1, h)
-        for h in halves:
-            product(0, CAND, 0, h)
+        for b in range(BLOCKS):
+            quantise_weights(CAND, 0, b)
+        products(0, CAND, 0)
 
-        def sigmoid(b, name, tag):
-            tile = keep.tile([P, S], F32, name=name, tag=tag, align_bytes=256)
-            for part in halves if b == 0 else [whole]:
-                nc.scalar.activation(out=tile[:, part], in_=acc[b, GATE, part.start][:], func=ACT.Sigmoid)
-            return tile
-
-        gate0 = sigmoid(0, "gate0", "w_raw1_0")
+        gates = keep.tile([P, BLOCKS, S], F32, name="gates", tag="w_raw1_0", align_bytes=256)
+        gate0, gate1 = gates[:, 0, :], gates[:, 1, :]
+        for h in halves:
+            nc.scalar.activation(out=gate0[:, h], in_=acc[0, GATE, h.start][:], func=ACT.Sigmoid)
+        nc.scalar.activation(out=gate1, in_=acc[1, GATE, 0][:], func=ACT.Sigmoid)
         for b in range(BLOCKS):
             round_weights(CAND, 1, b, True)
-        quantise_weights(CAND, 1, 0)
-        quantise_weights(CAND, 0, 1)
-        rest0 = keep.tile([P, S], F32, name="rest0", tag="w_grouped1_1_0", align_bytes=64)
-        nc.vector.tensor_scalar(out=rest0[:], in0=gate0[:], scalar1=-1.0, scalar2=1.0, op0=ALU.mult, op1=ALU.add)
-        for h in halves:
-            product(0, CAND, 1, h)
-        product(1, CAND, 0, whole)
-        for h in halves:
-            product(1, CAND, 1, h)
+        for b in range(BLOCKS):
+            quantise_weights(CAND, 1, b)
+        shared = keep.tile([P, 2 * S], F32, name="shared")
+        new0, term_b = shared[:, second], shared[:, S:]
+        begin = HALF - PIECE // 2
+        rest1 = shared[:, begin : 2 * S - begin].rearrange("p (g c) -> p g c", g=2)[:, :, :PIECE]
+        nc.vector.tensor_scalar(
+            out=rest1,
+            in0=gate1[:, :LEAD].rearrange("p (g c) -> p g c", g=2),
+            scalar1=-1.0,
+            scalar2=1.0,
+            op0=ALU.mult,
+            op1=ALU.add,
+        )
+        products(0, CAND, 1)
+        for z in reversed(range(PASSES)):
+            products(1, CAND, z)
 
-        old0 = keep.tile([P, HALF], F32, name="old0")
-        kept0 = keep.tile([P, S], F32, name="kept0")
+        old0 = keep.tile([P, S], F32, name="old0")
+        lost_first = keep.tile([P, HALF], F32, name="lost_first")
+        lost0 = [lost_first[:], shared[:, first]]
         fresh0 = keep.tile([P, S], F32, name="fresh0")
-        new0 = keep.tile([P, HALF], F32, name="new0")
-        old1 = keep.tile([P, S], F32, name="old1")
         gap1 = keep.tile([P, S], F32, name="gap1")
-        step1 = keep.tile([P, S], F32, name="step1")
+        term_a = keep.tile([P, S], F32, name="term_a")
+        lead, trail = slice(0, LEAD), slice(LEAD, S)
+        middle = (LEAD + S) // 2
+        trail_parts = [slice(LEAD, middle), slice(middle, S)]
 
         def look_up(dst, b, part):
             nc.scalar.activation(out=dst, in_=mem_sb[b][:].indirect(entries(slot_sb, part)), func=ACT.Copy)
 
-        first, second = halves
-        nc.vector.tensor_tensor(
-            kept0[:, first], mem_sb[0][:].indirect(entries(slot_sb, first)), rest0[:, first], ALU.mult
-        )
-        look_up(old0[:], 0, second)
-        gate1 = sigmoid(1, "gate1", "w_raw1_1")
+        def lose(h):
+            nc.vector.scalar_tensor_tensor(
+                out=lost0[h.start // HALF], in0=gate0[:, h], scalar=1.0, in1=old0[:, h], op0=ALU.subtract, op1=ALU.mult
+            )
+
         for h in halves:
-            look_up(old1[:, h], 1, h)
+            look_up(old0[:, h], 0, h)
+        look_up(term_b[:, trail], 1, trail)
         for h in halves:
             nc.vector.scalar_tensor_tensor(
                 out=fresh0[:, h], in0=acc[0, CAND, h.start][:], scalar=0.0, in1=gate0[:, h], op0=ALU.max, op1=ALU.mult
             )
-        nc.vector.tensor_tensor(new0[:], kept0[:, first], fresh0[:, first], ALU.add)
-        nc.vector.tensor_tensor(kept0[:, second], old0[:], rest0[:, second], ALU.mult)
-        nc.scalar.activation(out=mem_sb[0][:].indirect(entries(slot_sb, first)), in_=new0[:], func=ACT.Copy)
-        for h in halves:
-            nc.vector.scalar_tensor_tensor(
-                out=gap1[:, h], in0=acc[1, CAND, 0][:, h], scalar=0.0, in1=old1[:, h], op0=ALU.max, op1=ALU.subtract
+        lose(first)
+        for g in range(2):
+            piece = slice(g * PIECE, (g + 1) * PIECE)
+            nc.vector.tensor_tensor(
+                term_a[:, piece], mem_sb[1][:].indirect(entries(slot_sb, piece)), rest1[:, g, :], ALU.mult
             )
-        for h in halves:
-            nc.vector.tensor_tensor(step1[:, h], gap1[:, h], gate1[:, h], ALU.mult)
-        nc.vector.tensor_tensor(gap1[:, first], kept0[:, second], fresh0[:, second], ALU.add)
+        nc.vector.tensor_tensor(new0, fresh0[:, first], lost0[0], ALU.subtract)
+        nc.scalar.activation(out=mem_sb[0][:].indirect(entries(slot_sb, first)), in_=new0, func=ACT.Copy)
+        lose(second)
+        nc.vector.scalar_tensor_tensor(
+            out=term_b[:, lead], in0=acc[1, CAND, 0][:, lead], scalar=0.0, in1=gate1[:, lead], op0=ALU.max, op1=ALU.mult
+        )
+        gaps = [gap1[:, g * HALF : g * HALF + middle - LEAD] for g in range(2)]
+        for gap, part in zip(gaps, trail_parts):
+            nc.vector.scalar_tensor_tensor(
+                out=gap, in0=acc[1, CAND, 0][:, part], scalar=0.0, in1=term_b[:, part], op0=ALU.max, op1=ALU.subtract
+            )
+        for gap, part in zip(gaps, trail_parts):
+            nc.vector.tensor_tensor(term_a[:, part], gap, gate1[:, part], ALU.mult)
+        nc.vector.tensor_tensor(gap1[:, first], fresh0[:, second], lost0[1], ALU.subtract)
         nc.scalar.activation(out=mem_sb[0][:].indirect(entries(slot_sb, second)), in_=gap1[:, first], func=ACT.Copy)
         nc.sync.dma_start(out=out[0:P, :], in_=mem_sb[0][:])
-        nc.vector.tensor_tensor(mem_sb[1][:].indirect(slot_sb[:]), step1[:], old1[:], ALU.add)
+        nc.vector.tensor_tensor(mem_sb[1][:].indirect(slot_sb[:]), term_a[:], term_b[:], ALU.add)
         nc.sync.dma_start(out=out[P : 2 * P, :], in_=mem_sb[1][:])

@@ -22,7 +22,7 @@ PASSES = K // K_PASS
 BLOCKS = N // P
 GATE, CAND = 0, 1
 HALF = S // 2
-LEAD = 192
+LEAD = S // 4
 PIECE = LEAD // 2
 
 
@@ -190,13 +190,23 @@ def tile_picked_gmem_relu_e_kernel(tc, xT, mem, w1, w2, offs, slot, out):
             round_weights(CAND, 1, b, True)
         for b in range(BLOCKS):
             quantise_weights(CAND, 1, b)
-        shared = keep.tile([P, 2 * S], F32, name="shared")
-        new0, term_b = shared[:, second], shared[:, S:]
-        begin = HALF - PIECE // 2
-        rest1 = shared[:, begin : 2 * S - begin].rearrange("p (g c) -> p g c", g=2)[:, :, :PIECE]
+        lead, trail = slice(0, LEAD), slice(LEAD, S)
+        pieces = [slice(0, PIECE), slice(PIECE, LEAD)]
+        middle = (LEAD + S) // 2
+        trail_parts = [slice(LEAD, middle), slice(middle, S)]
+        fresh_first = keep.tile([P, HALF + PIECE], F32, name="fresh_first")
+        shared = keep.tile([P, 3 * HALF + S], F32, name="shared")
+        lost_first = keep.tile([P, HALF], F32, name="lost_first")
+        lost0 = [lost_first[:], shared[:, :HALF]]
+        new0 = shared[:, HALF : 2 * HALF]
+        fresh0 = [fresh_first[:, :HALF], shared[:, 2 * HALF : 3 * HALF]]
+        term_b = shared[:, 3 * HALF :]
+        short0 = fresh_first[:, HALF - PIECE :]
+        rest1 = shared[:, HALF - PIECE // 2 : HALF - PIECE // 2 + 2 * S].rearrange("p (g c) -> p g c", g=2)[:, :, :PIECE]
+        nc.vector.tensor_scalar(out=short0, in0=gate0[:, lead], scalar1=1.0, scalar2=-1.0, op0=ALU.mult, op1=ALU.add)
         nc.vector.tensor_scalar(
             out=rest1,
-            in0=gate1[:, :LEAD].rearrange("p (g c) -> p g c", g=2),
+            in0=gate1[:, lead].rearrange("p (g c) -> p g c", g=2),
             scalar1=-1.0,
             scalar2=1.0,
             op0=ALU.mult,
@@ -207,42 +217,46 @@ def tile_picked_gmem_relu_e_kernel(tc, xT, mem, w1, w2, offs, slot, out):
             products(1, CAND, z)
 
         old0 = keep.tile([P, S], F32, name="old0")
-        lost_first = keep.tile([P, HALF], F32, name="lost_first")
-        lost0 = [lost_first[:], shared[:, first]]
-        fresh0 = keep.tile([P, S], F32, name="fresh0")
         gap1 = keep.tile([P, S], F32, name="gap1")
         term_a = keep.tile([P, S], F32, name="term_a")
-        lead, trail = slice(0, LEAD), slice(LEAD, S)
-        middle = (LEAD + S) // 2
-        trail_parts = [slice(LEAD, middle), slice(middle, S)]
 
         def look_up(dst, b, part):
             nc.scalar.activation(out=dst, in_=mem_sb[b][:].indirect(entries(slot_sb, part)), func=ACT.Copy)
 
-        def lose(h):
+        def lose(dst, part):
             nc.vector.scalar_tensor_tensor(
-                out=lost0[h.start // HALF], in0=gate0[:, h], scalar=1.0, in1=old0[:, h], op0=ALU.subtract, op1=ALU.mult
+                out=dst, in0=gate0[:, part], scalar=1.0, in1=old0[:, part], op0=ALU.subtract, op1=ALU.mult
             )
 
-        for h in halves:
-            look_up(old0[:, h], 0, h)
-        look_up(term_b[:, trail], 1, trail)
-        for h in halves:
+        def freshen(dst, b, part):
+            bank = part.start if b == 0 else 0
             nc.vector.scalar_tensor_tensor(
-                out=fresh0[:, h], in0=acc[0, CAND, h.start][:], scalar=0.0, in1=gate0[:, h], op0=ALU.max, op1=ALU.mult
+                out=dst,
+                in0=acc[b, CAND, bank][:, part.start - bank : part.stop - bank],
+                scalar=0.0,
+                in1=gates[:, b, part],
+                op0=ALU.max,
+                op1=ALU.mult,
             )
-        lose(first)
-        for g in range(2):
-            piece = slice(g * PIECE, (g + 1) * PIECE)
+
+        for piece in pieces:
+            nc.vector.tensor_tensor(
+                lost_first[:, piece], mem_sb[0][:].indirect(entries(slot_sb, piece)), short0[:, piece], ALU.mult
+            )
+        for part in (slice(LEAD, HALF), second):
+            look_up(old0[:, part], 0, part)
+        look_up(term_b[:, trail], 1, trail)
+        freshen(fresh0[0], 0, first)
+        lose(lost_first[:, LEAD:], slice(LEAD, HALF))
+        for g, piece in enumerate(pieces):
             nc.vector.tensor_tensor(
                 term_a[:, piece], mem_sb[1][:].indirect(entries(slot_sb, piece)), rest1[:, g, :], ALU.mult
             )
-        nc.vector.tensor_tensor(new0, fresh0[:, first], lost0[0], ALU.subtract)
+        nc.vector.tensor_tensor(new0, fresh0[0], lost0[0], ALU.subtract)
         nc.scalar.activation(out=mem_sb[0][:].indirect(entries(slot_sb, first)), in_=new0, func=ACT.Copy)
-        lose(second)
-        nc.vector.scalar_tensor_tensor(
-            out=term_b[:, lead], in0=acc[1, CAND, 0][:, lead], scalar=0.0, in1=gate1[:, lead], op0=ALU.max, op1=ALU.mult
-        )
+        lose(lost0[1], second)
+        freshen(fresh0[1], 0, second)
+        freshen(term_b[:, lead], 1, lead)
         gaps = [gap1[:, g * HALF : g * HALF + middle - LEAD] for g in range(2)]
         for gap, part in zip(gaps, trail_parts):
             nc.vector.scalar_tensor_tensor(
@@ -250,7 +264,7 @@ def tile_picked_gmem_relu_e_kernel(tc, xT, mem, w1, w2, offs, slot, out):
             )
         for gap, part in zip(gaps, trail_parts):
             nc.vector.tensor_tensor(term_a[:, part], gap, gate1[:, part], ALU.mult)
-        nc.vector.tensor_tensor(gap1[:, first], fresh0[:, second], lost0[1], ALU.subtract)
+        nc.vector.tensor_tensor(gap1[:, first], fresh0[1], lost0[1], ALU.subtract)
         nc.scalar.activation(out=mem_sb[0][:].indirect(entries(slot_sb, second)), in_=gap1[:, first], func=ACT.Copy)
         nc.sync.dma_start(out=out[0:P, :], in_=mem_sb[0][:])
         nc.vector.tensor_tensor(mem_sb[1][:].indirect(slot_sb[:]), term_a[:], term_b[:], ALU.add)

@@ -74,13 +74,18 @@ def tile_picked_gmem_relu_e_kernel(tc, xT, mem, w1, w2, offs, slot, out):
         halves = [slice(0, HALF), slice(HALF, S)]
         first, second = halves
         x_words = [keep.tile([P, S], U32, name="x_words%d" % z, align_bytes=64) for z in range(PASSES)]
-        x_scales = [keep.tile([P, S], U8, name="x_scales%d" % z, align_bytes=64) for z in range(PASSES)]
+        scales0 = keep.tile([P, S], U8, name="x_scales0", align_bytes=64)
+        x_scales = {(0, part.start, part.stop): scales0[:, part] for part in halves + [whole]}
         x_grouped = [keep.tile([P, S * PACK], BF16, name="x_grouped%d" % z, align_bytes=64) for z in range(PASSES)]
 
         def quantise_messages(z, part):
+            if z == 1:
+                tag = "x_scales1" if part == first else "w_grouped0_0_1"
+                tile = keep.tile([P, HALF], U8, name="x_scales1_%d" % part.start, tag=tag, align_bytes=64)
+                x_scales[1, part.start, part.stop] = tile[:]
             nc.vector.quantize_mx(
                 out=x_words[z][:, part].bitcast(FP8X4),
-                scales=x_scales[z][:, part],
+                scales=x_scales[z, part.start, part.stop],
                 in_=x_grouped[z][:, part.start * PACK : part.stop * PACK],
             )
 
@@ -142,36 +147,41 @@ def tile_picked_gmem_relu_e_kernel(tc, xT, mem, w1, w2, offs, slot, out):
 
         acc = {}
 
-        def product(b, m, z, part):
-            opens = z == (1 if (b, m) == (1, CAND) else 0)
+        def product(b, m, z, part, bank, opens, closes):
             if opens:
-                acc[b, m, part.start] = psum.tile(
-                    [P, part.stop - part.start], F32, name="acc%d_%d_%d" % (b, m, part.start)
+                acc[b, m, bank.start] = psum.tile(
+                    [P, bank.stop - bank.start], F32, name="acc%d_%d_%d" % (b, m, bank.start)
                 )
             nc.tensor.matmul_mx(
-                out=acc[b, m, part.start][:],
+                out=acc[b, m, bank.start][:, part.start - bank.start : part.stop - bank.start],
                 lhsT=w_words[m, z, b].bitcast(FP8X4),
                 lhsT_scale=w_scales[m, z, b],
                 rhs=x_words[z][:, part].bitcast(FP8X4),
-                rhs_scale=x_scales[z][:, part],
+                rhs_scale=x_scales[z, part.start, part.stop],
                 start=opens,
-                stop=not opens,
+                stop=closes,
             )
 
         def products(b, m, z):
-            for part in halves if b == 0 else [whole]:
-                product(b, m, z, part)
+            if b == 0:
+                for h in halves:
+                    product(b, m, z, h, h, z == 0, z == 1)
+            elif z == 0:
+                product(b, m, z, whole, whole, m == GATE, m == CAND)
+            else:
+                for h in halves:
+                    product(b, m, z, h, whole, m == CAND and h == first, m == GATE and h == second)
 
         for b in range(BLOCKS):
             round_weights(GATE, 0, b, False)
-        for h in halves:
-            quantise_messages(1, h)
+        quantise_messages(1, first)
         quantise_weights(GATE, 0, 0)
         round_weights(GATE, 1, 0, True)
         round_weights(GATE, 1, 1, False)
         quantise_weights(GATE, 0, 1)
-        for b in range(BLOCKS):
-            quantise_weights(GATE, 1, b)
+        quantise_weights(GATE, 1, 0)
+        quantise_messages(1, second)
+        quantise_weights(GATE, 1, 1)
         for z in range(PASSES):
             for b in range(BLOCKS):
                 products(b, GATE, z)

@@ -57,8 +57,7 @@ def tile_picked_gmem_relu_e_kernel(tc, xT, mem, w1, w2, offs, slot, out):
                 rows = (w2, w1)[m][z * K_PASS : (z + 1) * K_PASS, :]
                 nc.sync.dma_start(out=raw[:], in_=rows.rearrange("(p j) c -> p (j c)", j=PACK))
                 w_raw[m, z] = raw[:].rearrange("p (u a c) -> p u a c", u=2, a=2)
-            if m == GATE:
-                nc.sync.dma_start(slot_sb[:], slot)
+        nc.sync.dma_start(slot_sb[:], slot)
         mem_sb = []
         for b in range(BLOCKS):
             mem_b = keep.tile([P, U], F32, name="mem%d" % b, align_bytes=256)
@@ -163,14 +162,14 @@ def tile_picked_gmem_relu_e_kernel(tc, xT, mem, w1, w2, offs, slot, out):
             )
 
         def products(b, m, z):
-            if b == 0:
+            if (b, m) != (1, CAND):
                 for h in halves:
                     product(b, m, z, h, h, z == 0, z == 1)
             elif z == 0:
-                product(b, m, z, whole, whole, m == GATE, m == CAND)
+                product(b, m, z, whole, whole, False, True)
             else:
                 for h in halves:
-                    product(b, m, z, h, whole, m == CAND and h == first, m == GATE and h == second)
+                    product(b, m, z, h, whole, h == first, False)
 
         for b in range(BLOCKS):
             round_weights(GATE, 0, b, False)
@@ -193,9 +192,9 @@ def tile_picked_gmem_relu_e_kernel(tc, xT, mem, w1, w2, offs, slot, out):
 
         gates = keep.tile([P, BLOCKS, S], F32, name="gates", tag="w_raw1_0", align_bytes=256)
         gate0, gate1 = gates[:, 0, :], gates[:, 1, :]
-        for h in halves:
-            nc.scalar.activation(out=gate0[:, h], in_=acc[0, GATE, h.start][:], func=ACT.Sigmoid)
-        nc.scalar.activation(out=gate1, in_=acc[1, GATE, 0][:], func=ACT.Sigmoid)
+        for b in range(BLOCKS):
+            for h in halves:
+                nc.scalar.activation(out=gates[:, b, h], in_=acc[b, GATE, h.start][:], func=ACT.Sigmoid)
         for b in range(BLOCKS):
             round_weights(CAND, 1, b, True)
         for b in range(BLOCKS):

@@ -203,16 +203,16 @@ def tile_picked_gmem_relu_e_kernel(tc, xT, mem, w1, w2, offs, slot, out):
         pieces = [slice(0, PIECE), slice(PIECE, LEAD)]
         middle = (LEAD + S) // 2
         trail_parts = [slice(LEAD, middle), slice(middle, S)]
-        fresh_first = keep.tile([P, HALF + PIECE], F32, name="fresh_first")
+        fresh_first = keep.tile([P, HALF + LEAD], F32, name="fresh_first")
         shared = keep.tile([P, 3 * HALF + S], F32, name="shared")
         lost_first = keep.tile([P, HALF], F32, name="lost_first")
         lost0 = [lost_first[:], shared[:, :HALF]]
         new0 = shared[:, HALF : 2 * HALF]
         fresh0 = [fresh_first[:, :HALF], shared[:, 2 * HALF : 3 * HALF]]
         term_b = shared[:, 3 * HALF :]
-        short0 = fresh_first[:, HALF - PIECE :]
+        short0 = fresh_first[:, HALF - LEAD :]
         rest1 = shared[:, HALF - PIECE // 2 : HALF - PIECE // 2 + 2 * S].rearrange("p (g c) -> p g c", g=2)[:, :, :PIECE]
-        nc.vector.tensor_scalar(out=short0, in0=gate0[:, lead], scalar1=1.0, scalar2=-1.0, op0=ALU.mult, op1=ALU.add)
+        nc.vector.tensor_scalar(out=short0, in0=gate0[:, first], scalar1=1.0, scalar2=-1.0, op0=ALU.mult, op1=ALU.add)
         nc.vector.tensor_scalar(
             out=rest1,
             in0=gate1[:, lead].rearrange("p (g c) -> p g c", g=2),
@@ -248,15 +248,13 @@ def tile_picked_gmem_relu_e_kernel(tc, xT, mem, w1, w2, offs, slot, out):
                 op1=ALU.mult,
             )
 
-        for piece in pieces:
+        for piece in (lead, slice(LEAD, HALF)):
             nc.vector.tensor_tensor(
                 lost_first[:, piece], mem_sb[0][:].indirect(entries(slot_sb, piece)), short0[:, piece], ALU.mult
             )
-        for part in (slice(LEAD, HALF), second):
-            look_up(old0[:, part], 0, part)
+        look_up(old0[:, second], 0, second)
         look_up(term_b[:, trail], 1, trail)
         freshen(fresh0[0], 0, first)
-        lose(lost_first[:, LEAD:], slice(LEAD, HALF))
         for g, piece in enumerate(pieces):
             nc.vector.tensor_tensor(
                 term_a[:, piece], mem_sb[1][:].indirect(entries(slot_sb, piece)), rest1[:, g, :], ALU.mult
@@ -265,12 +263,12 @@ def tile_picked_gmem_relu_e_kernel(tc, xT, mem, w1, w2, offs, slot, out):
         nc.scalar.activation(out=mem_sb[0][:].indirect(entries(slot_sb, first)), in_=new0, func=ACT.Copy)
         lose(lost0[1], second)
         freshen(fresh0[1], 0, second)
-        freshen(term_b[:, lead], 1, lead)
         gaps = [gap1[:, g * HALF : g * HALF + middle - LEAD] for g in range(2)]
         for gap, part in zip(gaps, trail_parts):
             nc.vector.scalar_tensor_tensor(
                 out=gap, in0=acc[1, CAND, 0][:, part], scalar=0.0, in1=term_b[:, part], op0=ALU.max, op1=ALU.subtract
             )
+        freshen(term_b[:, lead], 1, lead)
         for gap, part in zip(gaps, trail_parts):
             nc.vector.tensor_tensor(term_a[:, part], gap, gate1[:, part], ALU.mult)
         nc.vector.tensor_tensor(gap1[:, first], fresh0[1], lost0[1], ALU.subtract)

from contextlib import ExitStack

import concourse.mybir as mybir

K, T, S, N, U = 1024, 1024, 512, 256, 1024
FLOPS = 2 * 2 * K * N * S

F32 = mybir.dt.float32
BF16 = mybir.dt.bfloat16
U32 = mybir.dt.uint32
I32 = mybir.dt.int32
U16 = mybir.dt.uint16
U8 = mybir.dt.uint8
FP8X4 = mybir.dt.float8_e4m3fn_x4
ACT = mybir.ActivationFunctionType
ALU = mybir.AluOpType

P = 128
PACK = 4
K_PASS = P * PACK
PASSES = K // K_PASS
BLOCKS = N // P
GATE, CAND = 0, 1
HALF = S // 2
LEAD = S // 4
PIECE = LEAD // 2


def entries(list_sb, part):
    return list_sb[:, part.start // 16 : part.stop // 16]


def tile_picked_gmem_relu_e_kernel(tc, xT, mem, w1, w2, offs, slot, out):
    nc = tc.nc
    with ExitStack() as ctx:
        keep = ctx.enter_context(tc.tile_pool(name="keep", bufs=1))
        psum = ctx.enter_context(tc.psum_pool(name="psum", bufs=1))

        offs_sb = keep.tile([P, S // 16], U16, name="offs_sb")
        slot_sb = keep.tile([P, S // 16], U16, name="slot_sb")

        x_raw = {}
        rows = xT[:K_PASS, :].rearrange("(p u a) t -> p u (a t)", u=2, a=2)
        for u in range(2):
            x_raw[0, u] = keep.tile([P, 2 * T], F32, name="x_raw0_%d" % u, align_bytes=256)
            nc.sync.dma_start(out=x_raw[0, u][:], in_=rows[:, u, :])
            if u == 0:
                nc.sync.dma_start(offs_sb[:], offs)
        rows = xT[K_PASS:, :].rearrange("(p j) t -> p j t", j=PACK)
        for j in range(PACK):
            x_raw[1, j] = keep.tile([P, T], F32, name="x_raw1_%d" % j, align_bytes=256)
            nc.sync.dma_start(out=x_raw[1, j][:], in_=rows[:, j, :])
        w_raw = {}
        for m in (GATE, CAND):
            for z in range(PASSES):
                raw = keep.tile([P, PACK * N], F32, name="w_raw%d_%d" % (m, z), align_bytes=256)
                rows = (w2, w1)[m][z * K_PASS : (z + 1) * K_PASS, :]
                nc.sync.dma_start(out=raw[:], in_=rows.rearrange("(p j) c -> p (j c)", j=PACK))
                w_raw[m, z] = raw[:].rearrange("p (u a c) -> p u a c", u=2, a=2)
        nc.sync.dma_start(slot_sb[:], slot)
        mem_sb = []
        for b in range(BLOCKS):
            mem_b = keep.tile([P, U], F32, name="mem%d" % b, align_bytes=256)
            nc.sync.dma_start(out=mem_b[:], in_=mem[b * P : (b + 1) * P, :])
            mem_sb.append(mem_b)

        zero = keep.tile([P, 1], F32, name="zero")
        warm = keep.tile([P, 1], F32, name="warm")
        nc.vector.memset(zero[:], 0.0)
        nc.scalar.activation(out=warm[:], in_=zero[:], func=ACT.Sigmoid)

        whole = slice(0, S)
        halves = [slice(0, HALF), slice(HALF, S)]
        first, second = halves
        x_words = [keep.tile([P, S], U32, name="x_words%d" % z, align_bytes=64) for z in range(PASSES)]
        scales0 = keep.tile([P, S], U8, name="x_scales0", align_bytes=64)
        x_scales = {(0, part.start, part.stop): scales0[:, part] for part in halves + [whole]}
        x_grouped = [keep.tile([P, S * PACK], BF16, name="x_grouped%d" % z, align_bytes=64) for z in range(PASSES)]

        def quantise_messages(z, part):
            if z == 1:
                tag = "x_scales1" if part == first else "w_grouped0_0_1"
                tile = keep.tile([P, HALF], U8, name="x_scales1_%d" % part.start, tag=tag, align_bytes=64)
                x_scales[1, part.start, part.stop] = tile[:]
            nc.vector.quantize_mx(
                out=x_words[z][:, part].bitcast(FP8X4),
                scales=x_scales[z, part.start, part.stop],
                in_=x_grouped[z][:, part.start * PACK : part.stop * PACK],
            )

        for z in range(PASSES):
            pairs = [keep.tile([P, 2, HALF, 2], BF16, name="pairs%d_%d" % (z, h)) for h in range(2)]
            for u in range(2):
                for i in range(2):
                    if z == 0:
                        picked = entries(offs_sb, halves[i])
                        by_scalar = pairs[i][:, 0, :, u], x_raw[0, u][:].indirect(picked)
                        by_vector = pairs[i][:, 1, :, u], x_raw[0, u][:, T:].indirect(picked)
                    else:
                        plane = x_raw[1, 2 * u + i]
                        by_scalar = pairs[1][:, i, :, u], plane[:].indirect(entries(offs_sb, second))
                        by_vector = pairs[0][:, i, :, u], plane[:].indirect(entries(offs_sb, first))
                    nc.scalar.activation(out=by_scalar[0], in_=by_scalar[1], func=ACT.Copy)
                    nc.vector.tensor_copy(out=by_vector[0], in_=by_vector[1])
            for h in range(2):
                nc.vector.tensor_copy(
                    out=x_grouped[z][:, h * HALF * PACK : (h + 1) * HALF * PACK]
                    .bitcast(I32)
                    .rearrange("p (c a) -> p c a", a=2),
                    in_=pairs[h][:].rearrange("p a c u -> p (a c u)").bitcast(I32).rearrange("p (a c) -> p c a", a=2),
                )
            if z == 0:
                quantise_messages(0, whole)

        w_grouped = {}
        w_words = {}
        w_scales = {}
        w_tiles = {}
        groups = [[(m, z, b)] for m in (GATE, CAND) for z in range(PASSES) for b in range(BLOCKS)]
        for members in groups:
            name = "%d_%d_%d" % members[-1]
            width = len(members) * P
            grouped = keep.tile([P, width, PACK], BF16, name="w_grouped" + name, align_bytes=64)
            words = keep.tile([P, width], U32, name="w_words" + name, align_bytes=64)
            scales = keep.tile([P, width], U8, name="w_scales" + name, align_bytes=64)
            w_tiles[members[-1]] = grouped, words, scales
            for i, member in enumerate(members):
                cols = slice(i * P, (i + 1) * P)
                w_grouped[member] = grouped[:, cols, :]
                w_words[member] = words[:, cols]
                w_scales[member] = scales[:, cols]

        def round_weights(m, z, b, on_vector):
            dst = w_grouped[m, z, b].rearrange("p (c i) (a u) -> p c a u i", i=4, u=2)
            src = w_raw[m, z][:, :, :, b * P : (b + 1) * P].rearrange("p u a (c i) -> p c a u i", i=4)
            if on_vector:
                nc.vector.tensor_copy(out=dst, in_=src)
            else:
                nc.scalar.copy(out=dst, in_=src)

        def quantise_weights(m, z, b):
            grouped, words, scales = w_tiles[m, z, b]
            nc.vector.quantize_mx(
                out=words[:].bitcast(FP8X4), scales=scales[:], in_=grouped[:].rearrange("p c t -> p (c t)")
            )

        acc = {}

        def product(b, m, z, part, bank, opens, closes):
            if opens:
                acc[b, m, bank.start] = psum.tile(
                    [P, bank.stop - bank.start], F32, name="acc%d_%d_%d" % (b, m, bank.start)
                )
            nc.tensor.matmul_mx(
                out=acc[b, m, bank.start][:, part.start - bank.start : part.stop - bank.start],
                lhsT=w_words[m, z, b].bitcast(FP8X4),
                lhsT_scale=w_scales[m, z, b],
                rhs=x_words[z][:, part].bitcast(FP8X4),
                rhs_scale=x_scales[z, part.start, part.stop],
                start=opens,
                stop=closes,
            )

        def products(b, m, z):
            if (b, m) != (1, CAND):
                for h in halves:
                    product(b, m, z, h, h, z == 0, z == 1)
            elif z == 0:
                product(b, m, z, whole, whole, False, True)
            else:
                for h in halves:
                    product(b, m, z, h, whole, h == first, False)

        for b in range(BLOCKS):
            round_weights(GATE, 0, b, False)
        quantise_messages(1, first)
        quantise_weights(GATE, 0, 0)
        round_weights(GATE, 1, 0, True)
        round_weights(GATE, 1, 1, False)
        quantise_weights(GATE, 0, 1)
        quantise_weights(GATE, 1, 0)
        quantise_messages(1, second)
        quantise_weights(GATE, 1, 1)
        for z in range(PASSES):
            for b in range(BLOCKS):
                products(b, GATE, z)
        round_weights(CAND, 0, 0, True)
        round_weights(CAND, 0, 1, False)
        for b in range(BLOCKS):
            quantise_weights(CAND, 0, b)
        products(0, CAND, 0)

        gates = keep.tile([P, BLOCKS, S], F32, name="gates", tag="w_raw1_0", align_bytes=256)
        gate0, gate1 = gates[:, 0, :], gates[:, 1, :]
        for b in range(BLOCKS):
            for h in halves:
                nc.scalar.activation(out=gates[:, b, h], in_=acc[b, GATE, h.start][:], func=ACT.Sigmoid)
        for b in range(BLOCKS):
            round_weights(CAND, 1, b, True)
        for b in range(BLOCKS):
            quantise_weights(CAND, 1, b)
        lead, trail = slice(0, LEAD), slice(LEAD, S)
        pieces = [slice(0, PIECE), slice(PIECE, LEAD)]
        middle = (LEAD + S) // 2
        trail_parts = [slice(LEAD, middle), slice(middle, S)]
        fresh_first = keep.tile([P, HALF + LEAD], F32, name="fresh_first")
        shared = keep.tile([P, 3 * HALF + S], F32, name="shared")
        lost_first = keep.tile([P, HALF], F32, name="lost_first")
        lost0 = [lost_first[:], shared[:, :HALF]]
        new0 = shared[:, HALF : 2 * HALF]
        fresh0 = [fresh_first[:, :HALF], shared[:, 2 * HALF : 3 * HALF]]
        term_b = shared[:, 3 * HALF :]
        short0 = fresh_first[:, HALF - LEAD :]
        rest1 = shared[:, HALF - PIECE // 2 : HALF - PIECE // 2 + 2 * S].rearrange("p (g c) -> p g c", g=2)[:, :, :PIECE]
        nc.vector.tensor_scalar(out=short0, in0=gate0[:, first], scalar1=1.0, scalar2=-1.0, op0=ALU.mult, op1=ALU.add)
        nc.vector.tensor_scalar(
            out=rest1,
            in0=gate1[:, lead].rearrange("p (g c) -> p g c", g=2),
            scalar1=-1.0,
            scalar2=1.0,
            op0=ALU.mult,
            op1=ALU.add,
        )
        products(0, CAND, 1)
        for z in reversed(range(PASSES)):
            products(1, CAND, z)

        old0 = keep.tile([P, S], F32, name="old0")
        gap1 = keep.tile([P, S], F32, name="gap1")
        term_a = keep.tile([P, S], F32, name="term_a")

        def look_up(dst, b, part):
            nc.scalar.activation(out=dst, in_=mem_sb[b][:].indirect(entries(slot_sb, part)), func=ACT.Copy)

        def lose(dst, part):
            nc.vector.scalar_tensor_tensor(
                out=dst, in0=gate0[:, part], scalar=1.0, in1=old0[:, part], op0=ALU.subtract, op1=ALU.mult
            )

        def freshen(dst, b, part):
            bank = part.start if b == 0 else 0
            nc.vector.scalar_tensor_tensor(
                out=dst,
                in0=acc[b, CAND, bank][:, part.start - bank : part.stop - bank],
                scalar=0.0,
                in1=gates[:, b, part],
                op0=ALU.max,
                op1=ALU.mult,
            )

        for piece in (lead, slice(LEAD, HALF)):
            nc.vector.tensor_tensor(
                lost_first[:, piece], mem_sb[0][:].indirect(entries(slot_sb, piece)), short0[:, piece], ALU.mult
            )
        look_up(old0[:, second], 0, second)
        look_up(term_b[:, trail], 1, trail)
        freshen(fresh0[0], 0, first)
        for g, piece in enumerate(pieces):
            nc.vector.tensor_tensor(
                term_a[:, piece], mem_sb[1][:].indirect(entries(slot_sb, piece)), rest1[:, g, :], ALU.mult
            )
        nc.vector.tensor_tensor(new0, fresh0[0], lost0[0], ALU.subtract)
        nc.scalar.activation(out=mem_sb[0][:].indirect(entries(slot_sb, first)), in_=new0, func=ACT.Copy)
        lose(lost0[1], second)
        freshen(fresh0[1], 0, second)
        gaps = [gap1[:, g * HALF : g * HALF + middle - LEAD] for g in range(2)]
        for gap, part in zip(gaps, trail_parts):
            nc.vector.scalar_tensor_tensor(
                out=gap, in0=acc[1, CAND, 0][:, part], scalar=0.0, in1=term_b[:, part], op0=ALU.max, op1=ALU.subtract
            )
        freshen(term_b[:, lead], 1, lead)
        for gap, part in zip(gaps, trail_parts):
            nc.vector.tensor_tensor(term_a[:, part], gap, gate1[:, part], ALU.mult)
        nc.vector.tensor_tensor(gap1[:, first], fresh0[1], lost0[1], ALU.subtract)
        nc.scalar.activation(out=mem_sb[0][:].indirect(entries(slot_sb, second)), in_=gap1[:, first], func=ACT.Copy)
        nc.sync.dma_start(out=out[0:P, :], in_=mem_sb[0][:])
        nc.vector.tensor_tensor(mem_sb[1][:].indirect(slot_sb[:]), term_a[:], term_b[:], ALU.add)
        nc.sync.dma_start(out=out[P : 2 * P, :], in_=mem_sb[1][:])
